import numpy as np
import ml_dtypes


def mxq(x, axis, fmt="e4m3"):
    dtype, down = {"e4m3": (ml_dtypes.float8_e4m3fn, 7), "e5m2": (ml_dtypes.float8_e5m2, 14)}[fmt]
    v = np.moveaxis(np.asarray(x, np.float32).astype(ml_dtypes.bfloat16).astype(np.float64), axis, -1)
    blocks = v.reshape(v.shape[:-1] + (-1, 32))
    amax = np.abs(blocks).max(-1, keepdims=True)
    byte = np.maximum(np.where(amax > 0, np.frexp(amax)[1] - 1 + 127, 0) - down, 1)
    scale = np.exp2(byte - 127.0)
    codes = (blocks / scale).astype(np.float32).astype(dtype).astype(np.float64)
    return np.moveaxis((codes * scale).reshape(v.shape), -1, axis)


WIDE = False


def mx_kscale(k):
    if not WIDE:
        return np.ones(k)
    levels = np.array([10, -10, 5, -5, 0])
    if k % 512:
        return np.exp2(np.random.permutation(np.resize(levels, k // 32))).repeat(32)
    a = np.empty((k // 512, 16))
    for p in range(k // 512):
        a[p, :8] = np.random.permutation(np.resize(levels, 8))
        for g in range(8):
            far = levels[np.abs(levels - a[p, g]) >= 10]
            a[p, g + 8] = far[np.random.randint(len(far))]
    return np.exp2(a.ravel()).repeat(32)


BF16 = ml_dtypes.bfloat16


def bf(x):
    return np.asarray(x, np.float32).astype(BF16)


def f64(x):
    return np.asarray(x).astype(np.float64)


M, E, K, D = 1024, 2048, 1024, 512


def draw0():
    s, t, u = mx_kscale(K), mx_kscale(E), mx_kscale(M)
    return {"mentions": bf(np.random.standard_normal((M, K)) * s),
            "entities": bf(np.random.standard_normal((E, K)) / np.sqrt(K) / s),
            "sharpness": bf(1 + 0.1 * np.random.standard_normal(M)),
            "prior": bf(0.5 * np.random.standard_normal(E)),
            "nil": bf(0.5 * np.random.standard_normal(M)),
            "rarity": bf((1 + 0.2 * np.random.standard_normal(E)) * t),
            "salience": bf((1 + 0.2 * np.random.standard_normal(M)) * u),
            "cards": bf(np.random.standard_normal((E, D)) / np.sqrt(E) / t[:, None]),
            "contexts": bf(np.random.standard_normal((M, D)) / np.sqrt(M) / u[:, None]),
            "nil_card": bf(np.random.standard_normal(D))}


def core(mentions, entities, sharpness, prior, nil, rarity, salience, cards, contexts, nil_card):
    score = mxq(f64(mentions), 1, "e4m3") @ mxq(f64(entities), 1, "e4m3").T
    z = score * f64(sharpness)[:, None] + f64(prior)[None, :]
    nl = f64(nil)
    c = np.maximum(np.max(z, axis=1), nl)
    e = np.exp(z - c[:, None])
    en = np.exp(nl - c)
    den = np.mean(e, axis=1) + en
    lift = e / den[:, None]
    p_nil = en / den
    by_entity = lift * f64(rarity)[None, :]
    linked = mxq(by_entity, 1, "e4m3") @ mxq(f64(cards), 0, "e4m3")
    linked = linked + p_nil[:, None] * f64(nil_card)[None, :]
    by_mention = lift * f64(salience)[:, None]
    profile = mxq(by_mention, 0, "e4m3").T @ mxq(f64(contexts), 0, "e4m3")
    return linked, profile


def e4m3fn_bytes(y):
    return np.clip(np.asarray(y, np.float64), -448.0, 448.0).astype(np.float32).astype(ml_dtypes.float8_e4m3fn).view(np.uint8)


def e4m3fn_values(b):
    return np.asarray(b, np.uint8).view(ml_dtypes.float8_e4m3fn).astype(np.float64)


def setup_inputs():
    d = draw0()
    x0 = np.asarray(d['entities']).astype(np.float64)
    s = (np.max(np.abs(x0), axis=(0,), keepdims=True) / 448.0).astype(np.float32)
    out = {}
    for k, v in d.items():
        if k == 'entities':
            out['entities_bytes'] = e4m3fn_bytes(x0 / s.astype(np.float64))
            out['entities_scale'] = s
        else:
            out[k] = v
    return out


def reference(mentions, entities_bytes, entities_scale, sharpness, prior, nil, rarity, salience, cards, contexts, nil_card):
    return core(mentions, e4m3fn_values(entities_bytes) * entities_scale.astype(np.float64), sharpness, prior, nil, rarity, salience, cards, contexts, nil_card)

@@ -1,0 +1,705 @@
+from contextlib import ExitStack
+
+import concourse.mybir as mybir
+from concourse.masks import make_identity
+
+M, E, K, D = 1024, 2048, 1024, 512
+FLOPS = 2 * M * E * (K + D + D)
+
+F32 = mybir.dt.float32
+BF16 = mybir.dt.bfloat16
+U32 = mybir.dt.uint32
+U8 = mybir.dt.uint8
+FP8 = mybir.dt.float8_e4m3fn
+FP8X4 = mybir.dt.float8_e4m3fn_x4
+ALU = mybir.AluOpType
+ACT = mybir.ActivationFunctionType
+ENG = mybir.EngineType
+
+P = 128
+G_M = M // 512
+G_E = E // 512
+KP = K // 512
+
+
+def quantize(nc, codes, scales, grouped):
+    nc.vector.quantize_mx(out=codes.bitcast(FP8X4), scales=scales, in_=grouped)
+
+
+def tile_entity_linking_lift_f6_kernel(
+    tc, mentions, entities_bytes, entities_scale, sharpness, prior, nil, rarity, salience,
+    cards, contexts, nil_card, out_0, out_1,
+):
+    nc = tc.nc
+    with ExitStack() as ctx:
+        const = ctx.enter_context(tc.tile_pool(name="const", bufs=1))
+        keep = ctx.enter_context(tc.tile_pool(name="keep", bufs=1))
+        work = ctx.enter_context(tc.tile_pool(name="work", bufs=2))
+        small = ctx.enter_context(tc.tile_pool(name="small", bufs=4))
+        psum = ctx.enter_context(tc.psum_pool(name="psum", bufs=3))
+        ctx.enter_context(tc.manual_schedule(engines={ENG.PE, ENG.Activation, ENG.DVE, ENG.Pool}))
+
+        scale_b = const.tile([P, K], F32)
+        sharp_h = const.tile([P, G_M, 4], BF16)
+        nil_h = const.tile([P, G_M, 4], BF16)
+        sal_h = const.tile([P, G_M, 4], BF16)
+        nc.scalar.dma_start(out=scale_b[:], in_=entities_scale.rearrange("o k -> (o k)").partition_broadcast(P))
+        warm = const.tile([P, 1], F32)
+        nc.vector.memset(warm[:], 0.0)
+        nc.scalar.activation(out=warm[:], in_=warm[:], func=ACT.Exp)
+        ident = const.tile([P, P], F32)
+        make_identity(nc, ident[:])
+        ebytes = []
+        for c in range(G_E):
+            eb = keep.tile([P, 4, K], U8, tag="eb", bufs=4)
+            ebytes.append(eb)
+        mraws = []
+        for g in range(G_M):
+            mraw = work.tile([P, 4, K], BF16, tag="big", bufs=4, align_bytes=64)
+            mraws.append(mraw)
+
+        def load_entities(c, j0, j1):
+            rows = entities_bytes.rearrange("(r p) k -> p r k", p=P)
+            nc.sync.dma_start(out=ebytes[c][:, j0:j1, :], in_=rows[:, 4 * c + j0 : 4 * c + j1, :])
+
+        def load_mentions(g):
+            nc.sync.dma_start(out=mraws[g][:], in_=mentions.rearrange("(g p t) k -> g p t k", p=P, t=4)[g])
+
+        load_entities(0, 0, 1)
+        load_entities(0, 1, 4)
+        load_mentions(0)
+        load_entities(1, 0, 4)
+        prior_b = const.tile([P, E], BF16)
+        rarity_b = const.tile([P, E], BF16)
+        nilc_b = const.tile([P, D], BF16)
+        nc.gpsimd.dma_start(out=sharp_h[:], in_=sharpness.rearrange("(g p t) -> p g t", p=P, t=4))
+        nc.gpsimd.dma_start(out=nil_h[:], in_=nil.rearrange("(g p t) -> p g t", p=P, t=4))
+        nc.gpsimd.dma_start(out=sal_h[:], in_=salience.rearrange("(g p t) -> p g t", p=P, t=4))
+        nc.sync.dma_start(out=prior_b[:], in_=prior.partition_broadcast(P))
+        load_entities(2, 0, 4)
+        load_entities(3, 0, 4)
+
+        sharp = const.tile([P, G_M * 4], F32)
+        nilv = const.tile([P, G_M * 4], F32)
+        nneg = const.tile([P, G_M * 4], F32)
+        sal = const.tile([P, G_M * 4], F32)
+        nc.gpsimd.tensor_copy(out=sharp[:], in_=sharp_h[:].rearrange("p g t -> p (g t)"))
+        nc.gpsimd.tensor_copy(out=nilv[:], in_=nil_h[:].rearrange("p g t -> p (g t)"))
+        nc.gpsimd.tensor_scalar(out=nneg[:], in0=nilv[:], scalar1=-1.0, scalar2=0.0, op0=ALU.mult, op1=ALU.add)
+        nc.gpsimd.tensor_copy(out=sal[:], in_=sal_h[:].rearrange("p g t -> p (g t)"))
+
+        craws = []
+        for g in range(G_E + G_M):
+            craw = work.tile([P, 4, D], BF16, tag="craw", bufs=3)
+            source = cards if g < G_E else contexts
+            nc.sync.dma_start(out=craw[:], in_=source.rearrange("(g p t) d -> g p t d", p=P, t=4)[g % G_E])
+            craws.append(craw)
+        nc.sync.dma_start(out=rarity_b[:], in_=rarity.partition_broadcast(P))
+        load_mentions(1)
+        nc.sync.dma_start(out=nilc_b[:], in_=nil_card.partition_broadcast(P))
+
+        S = {}
+
+        def transpose_rows(rows):
+            words = rows.bitcast(F32)
+            xt = psum.tile([P, KP, 2, P], F32, tag="tr", bufs=3)
+            for c in range(KP):
+                for u in range(2):
+                    nc.tensor.transpose(xt[:, c, u, :], words[:, 256 * c + u : 256 * (c + 1) : 2], ident[:])
+            return xt
+
+        def copy_rows(xt, grouped):
+            nc.scalar.copy(out=grouped, in_=xt[:].rearrange("p c u r -> p c r u"))
+
+        mgs, mq, mqs = [], [], []
+
+        def mention_rows(g, t):
+            if t == 0:
+                mg = work.tile([P, 4, KP, P, 4], BF16, tag="big", bufs=4, align_bytes=64)
+                mgs.append(mg)
+            grouped = mgs[g][:, t].rearrange("p c r j -> p (c r j)").bitcast(F32).rearrange("p (c r u) -> p c r u", c=KP, u=2)
+            S["mt", g, t] = transpose_rows(mraws[g][:, t, :]), grouped
+
+        def mention_copy(g, t):
+            copy_rows(*S["mt", g, t])
+
+        def mention_codes(g):
+            codes = keep.tile([P, 4 * KP * P], U32, tag="mq", bufs=2, align_bytes=64)
+            scales = keep.tile([P, 4 * KP * P], U8, tag="mqs", bufs=2, align_bytes=64)
+            quantize(nc, codes[:], scales[:], mgs[g][:].rearrange("p t c r j -> p (t c r j)"))
+            mq.append(codes)
+            mqs.append(scales)
+
+        egs, xbs, eq, eqs = [], {}, [], []
+
+        def entity_scale(c, q):
+            if q == 0:
+                eg = work.tile([P, KP, 4, P, 4], BF16, tag="big", bufs=4, align_bytes=64)
+                egs.append(eg)
+            xb = work.tile([P, K], BF16, tag="xb", bufs=3)
+            nc.vector.tensor_tensor(out=xb[:], in0=ebytes[c][:, q, :].bitcast(FP8), in1=scale_b[:], op=ALU.mult)
+            xbs[c, q] = xb
+
+        def entity_rows(c, q):
+            egw = egs[c][:].rearrange("p c q r j -> p (c q r j)").bitcast(F32).rearrange("p (c q r u) -> p c q r u", c=KP, q=4, u=2)
+            S["et", c, q] = transpose_rows(xbs[c, q][:]), egw[:, :, q]
+
+        def entity_copy(c, q):
+            copy_rows(*S["et", c, q])
+
+        def entity_codes(c):
+            codes = keep.tile([P, KP * 512], U32, tag="eq", bufs=4, align_bytes=64)
+            scales = keep.tile([P, KP * 512], U8, tag="eqs", bufs=4, align_bytes=64)
+            quantize(nc, codes[:], scales[:], egs[c][:].rearrange("p c q r j -> p (c q r j)"))
+            eq.append(codes)
+            eqs.append(scales)
+
+        cgs, cq, cqs = [], [], []
+
+        def card_part(g, part):
+            if part == 0:
+                cg = work.tile([P, D, 4], BF16, tag="grp", bufs=4, align_bytes=64)
+                cgs.append(cg)
+            cols = slice(part * 128, (part + 1) * 128)
+            nc.scalar.copy(out=cgs[g][:, cols, :], in_=craws[g][:, :, cols].rearrange("p t d -> p d t"))
+
+        def card_codes(g):
+            codes = keep.tile([P, D], U32, tag="cq", bufs=6, align_bytes=64)
+            scales = keep.tile([P, D], U8, tag="cqs", bufs=6, align_bytes=64)
+            quantize(nc, codes[:], scales[:], cgs[g][:].rearrange("p d j -> p (d j)"))
+            cq.append(codes)
+            cqs.append(scales)
+
+        bmq, bmqs, bmp = [], [], []
+        for g in range(G_M):
+            codes = keep.tile([P, E], U32, tag="bmq", bufs=2, align_bytes=64)
+            scales = keep.tile([P, E], U8, tag="bmqs", bufs=2, align_bytes=64)
+            bmq.append(codes)
+            bmqs.append(scales)
+            pairs = work.tile([P, 2, E, 2], BF16, tag="bmp", bufs=1)
+            bmp.append(pairs)
+
+        def score(i, c):
+            g, t = divmod(i, 4)
+            sc = psum.tile([P, 512], F32, tag="sc", bufs=3)
+            for k in range(KP):
+                lo = (t * KP + k) * P
+                nc.tensor.matmul_mx(
+                    out=sc[:],
+                    lhsT=mq[g][:, lo : lo + P].bitcast(FP8X4), lhsT_scale=mqs[g][:, lo : lo + P],
+                    rhs=eq[c][:, k * 512 : (k + 1) * 512].bitcast(FP8X4), rhs_scale=eqs[c][:, k * 512 : (k + 1) * 512],
+                    start=(k == 0), stop=(k == KP - 1),
+                )
+            S["sc", i, c] = sc
+
+        def logit(i, c):
+            if c == 0:
+                z = work.tile([P, E], F32, tag="z", bufs=3)
+                zb = work.tile([P, E], BF16, tag="zb", bufs=2)
+                S["z", i], S["zb", i] = z, zb
+            cols = slice(c * 512, (c + 1) * 512)
+            nc.vector.scalar_tensor_tensor(
+                out=S["z", i][:, cols], in0=S["sc", i, c][:], scalar=sharp[:, i : i + 1],
+                in1=prior_b[:, cols], op0=ALU.mult, op1=ALU.add,
+            )
+
+        def coarse(i, c):
+            cols = slice(c * 512, (c + 1) * 512)
+            nc.scalar.activation(out=S["zb", i][:, cols], in_=S["z", i][:, cols], func=ACT.Copy, scale=-1.0)
+
+        def peak(i):
+            zb = S["zb", i]
+            negc = small.tile([P, 1], F32)
+            nc.vector.tensor_scalar(out=zb[:], in0=zb[:], scalar1=1.0, scalar2=nneg[:, i : i + 1], op0=ALU.mult, op1=ALU.min, accum_out=negc[:])
+            S["negc", i] = negc
+
+        def expo(i):
+            z, negc = S["z", i], S["negc", i]
+            total = small.tile([P, 1], F32)
+            en = small.tile([P, 1], F32)
+            nc.scalar.activation(out=en[:], in_=nilv[:, i : i + 1], func=ACT.Exp, bias=negc[:])
+            nc.scalar.activation(out=z[:], in_=z[:], func=ACT.Exp, bias=negc[:], accum_out=total[:])
+            S["total", i], S["en", i] = total, en
+
+        def denominator(i):
+            den = small.tile([P, 1], F32)
+            nc.vector.scalar_tensor_tensor(out=den[:], in0=S["total", i][:], scalar=1.0 / E, in1=S["en", i][:], op0=ALU.mult, op1=ALU.add)
+            S["den", i] = den
+
+        def ratio(i):
+            rden = small.tile([P, 1], F32)
+            nc.vector.reciprocal(out=rden[:], in_=S["den", i][:])
+            S["rden", i] = rden
+
+        def salient(i):
+            fsal = small.tile([P, 1], F32)
+            nc.gpsimd.tensor_tensor(out=fsal[:], in0=sal[:, i : i + 1], in1=S["rden", i][:], op=ALU.mult)
+            S["fsal", i] = fsal
+
+        def by_mention(i, j, n, eng):
+            g, t = divmod(i, 4)
+            z, fsal = S["z", i], S["fsal", i]
+            cols = slice(j * n, (j + 1) * n)
+            dst = bmp[g][:, t // 2, cols, t % 2]
+            if eng == "G":
+                nc.gpsimd.tensor_scalar(out=dst, in0=z[:, cols], scalar1=fsal[:], scalar2=0.0, op0=ALU.mult, op1=ALU.add)
+            else:
+                nc.scalar.activation(out=dst, in_=z[:, cols], func=ACT.Copy, scale=fsal[:])
+
+        def nil_share(i):
+            pnil = small.tile([P, 1], F32)
+            nc.gpsimd.tensor_tensor(out=pnil[:], in0=S["en", i][:], in1=S["rden", i][:], op=ALU.mult)
+            S["pnil", i] = pnil
+
+        def by_entity(i):
+            be = work.tile([P, E], BF16, tag="be", bufs=2)
+            nc.vector.scalar_tensor_tensor(
+                out=be[:], in0=S["z", i][:], scalar=S["rden", i][:], in1=rarity_b[:], op0=ALU.mult, op1=ALU.mult,
+            )
+            S["be", i] = be
+
+        def turn(i, h):
+            if h == 0:
+                bg = work.tile([P, G_E, P, 4], BF16, tag="grp", bufs=4, align_bytes=64)
+                S["bg", i] = bg
+            words = S["be", i][:].bitcast(F32)
+            bgw = S["bg", i][:].rearrange("p c r j -> p (c r j)").bitcast(F32).rearrange("p (c r u) -> p c r u", c=G_E, u=2)
+            xt = psum.tile([P, 2, 2, P], F32, tag="tr", bufs=3)
+            for c in range(2):
+                for u in range(2):
+                    lo = 256 * (2 * h + c)
+                    nc.tensor.transpose(xt[:, c, u, :], words[:, lo + u : lo + 256 : 2], ident[:])
+            S["xt", i, h] = xt, bgw
+
+        def turn_copy(i, h):
+            xt, bgw = S["xt", i, h]
+            nc.scalar.copy(out=bgw[:, 2 * h : 2 * h + 2], in_=xt[:].rearrange("p c u r -> p c r u"))
+
+        def entity_quant(i):
+            codes = work.tile([P, G_E * P], U32, tag="beq", bufs=2, align_bytes=64)
+            scales = work.tile([P, G_E * P], U8, tag="beqs", bufs=2, align_bytes=64)
+            quantize(nc, codes[:], scales[:], S["bg", i][:].rearrange("p c r j -> p (c r j)"))
+            S["beq", i] = codes, scales
+
+        def linked(i):
+            codes, scales = S["beq", i]
+            acc = psum.tile([P, D], F32, tag="acc", bufs=2)
+            for c in range(G_E):
+                nc.tensor.matmul_mx(
+                    out=acc[:],
+                    lhsT=codes[:, c * P : (c + 1) * P].bitcast(FP8X4), lhsT_scale=scales[:, c * P : (c + 1) * P],
+                    rhs=cq[c][:].bitcast(FP8X4), rhs_scale=cqs[c][:],
+                    start=(c == 0), stop=(c == G_E - 1),
+                )
+            S["acc", i] = acc
+
+        def linked_out(i):
+            g, t = divmod(i, 4)
+            res = work.tile([P, D], F32, tag="res", bufs=4)
+            nc.vector.scalar_tensor_tensor(out=res[:], in0=nilc_b[:], scalar=S["pnil", i][:], in1=S["acc", i][:], op0=ALU.mult, op1=ALU.add)
+            nc.sync.dma_start(out=out_0.rearrange("(g p t) d -> g t p d", p=P, t=4)[g, t], in_=res[:])
+
+        def gather(g, c, eng):
+            bmi = work.tile([P, 512, 4], BF16, tag="grp", bufs=4, align_bytes=64)
+            src = bmp[g][:, :, c * 512 : (c + 1) * 512, :].rearrange("p u e v -> p u (e v)").bitcast(F32).rearrange("p u e -> p e u")
+            dst = bmi[:].rearrange("p e j -> p (e j)").bitcast(F32).rearrange("p (e u) -> p e u", u=2)
+            if eng == "V":
+                nc.vector.tensor_copy(out=dst, in_=src)
+            else:
+                nc.scalar.copy(out=dst, in_=src)
+            S["bmi", g, c] = bmi
+
+        def gather_quant(g, c):
+            cols = slice(c * 512, (c + 1) * 512)
+            quantize(nc, bmq[g][:, cols], bmqs[g][:, cols], S["bmi", g, c][:].rearrange("p e j -> p (e j)"))
+
+        def profile(r, tag):
+            acc = psum.tile([P, D], F32, tag=tag, bufs={"acc": 2, "sc": 3, "tr": 3}[tag])
+            cols = slice(r * P, (r + 1) * P)
+            for g in range(G_M):
+                nc.tensor.matmul_mx(
+                    out=acc[:],
+                    lhsT=bmq[g][:, cols].bitcast(FP8X4), lhsT_scale=bmqs[g][:, cols],
+                    rhs=cq[G_E + g][:].bitcast(FP8X4), rhs_scale=cqs[G_E + g][:],
+                    start=(g == 0), stop=(g == G_M - 1),
+                )
+            S["prof", r] = acc
+
+        def profile_out(r, eng):
+            if r % 4 == 0:
+                wide = work.tile([P, 4, D], F32, tag="z", bufs=3)
+                S["wide", r // 4] = wide
+            res = S["wide", r // 4][:, r % 4, :]
+            if eng == "S":
+                nc.scalar.copy(out=res, in_=S["prof", r][:])
+            else:
+                nc.vector.tensor_copy(out=res, in_=S["prof", r][:])
+            nc.sync.dma_start(out=out_1[r * P : (r + 1) * P, :], in_=res)
+
+        entity_scale(0, 0)
+        entity_scale(0, 1)
+        entity_rows(0, 0)
+        entity_copy(0, 0)
+        entity_scale(0, 2)
+        entity_rows(0, 1)
+        entity_copy(0, 1)
+        entity_scale(0, 3)
+        mention_rows(0, 0)
+        mention_copy(0, 0)
+        mention_rows(0, 1)
+        mention_copy(0, 1)
+        entity_rows(0, 2)
+        entity_scale(1, 0)
+        entity_copy(0, 2)
+        mention_rows(0, 2)
+        mention_copy(0, 2)
+        entity_rows(0, 3)
+        entity_scale(1, 1)
+        entity_copy(0, 3)
+        mention_rows(0, 3)
+        mention_copy(0, 3)
+        entity_rows(1, 0)
+        entity_codes(0)
+        entity_copy(1, 0)
+        entity_rows(1, 1)
+        entity_copy(1, 1)
+        mention_codes(0)
+        card_part(0, 0)
+        entity_scale(1, 2)
+        card_part(0, 1)
+        score(0, 0)
+        card_part(0, 2)
+        score(1, 0)
+        entity_scale(1, 3)
+        card_part(0, 3)
+        entity_rows(1, 2)
+        card_part(1, 0)
+        logit(0, 0)
+        entity_copy(1, 2)
+        entity_rows(1, 3)
+        logit(1, 0)
+        entity_copy(1, 3)
+        entity_scale(2, 0)
+        coarse(0, 0)
+        coarse(1, 0)
+        entity_codes(1)
+        card_part(1, 1)
+        entity_rows(2, 0)
+        entity_copy(2, 0)
+        entity_scale(2, 1)
+        card_part(1, 2)
+        score(0, 1)
+        score(1, 1)
+        card_part(1, 3)
+        card_codes(0)
+        card_part(2, 0)
+        entity_scale(2, 2)
+        entity_rows(2, 1)
+        entity_copy(2, 1)
+        logit(0, 1)
+        card_part(2, 1)
+        entity_rows(2, 2)
+        logit(1, 1)
+        card_part(2, 2)
+        entity_scale(2, 3)
+        entity_copy(2, 2)
+        coarse(0, 1)
+        entity_scale(3, 0)
+        coarse(1, 1)
+        entity_rows(2, 3)
+        entity_copy(2, 3)
+        card_codes(1)
+        card_part(2, 3)
+        entity_rows(3, 0)
+        entity_codes(2)
+        entity_copy(3, 0)
+        card_part(3, 0)
+        entity_scale(3, 1)
+        card_part(3, 1)
+        score(0, 2)
+        card_part(3, 2)
+        score(1, 2)
+        entity_scale(3, 2)
+        card_part(3, 3)
+        entity_rows(3, 1)
+        entity_copy(3, 1)
+        entity_scale(3, 3)
+        entity_rows(3, 2)
+        card_part(4, 0)
+        card_codes(2)
+        entity_copy(3, 2)
+        entity_rows(3, 3)
+        logit(0, 2)
+        card_part(4, 1)
+        logit(1, 2)
+        entity_copy(3, 3)
+        card_codes(3)
+        coarse(0, 2)
+        score(2, 0)
+        entity_codes(3)
+        coarse(1, 2)
+        card_part(4, 2)
+        mention_rows(1, 0)
+        logit(2, 0)
+        mention_copy(1, 0)
+        score(0, 3)
+        card_part(4, 3)
+        logit(0, 3)
+        score(1, 3)
+        card_part(5, 0)
+        logit(1, 3)
+        score(2, 3)
+        coarse(0, 3)
+        logit(2, 3)
+        score(2, 1)
+        coarse(1, 3)
+        score(2, 2)
+        peak(0)
+        card_part(5, 1)
+        score(3, 2)
+        card_part(5, 2)
+        peak(1)
+        mention_rows(1, 3)
+        expo(0)
+        logit(2, 1)
+        logit(2, 2)
+        score(3, 0)
+        card_codes(4)
+        expo(1)
+        score(3, 1)
+        denominator(0)
+        ratio(0)
+        salient(0)
+        by_entity(0)
+        nil_share(0)
+        by_mention(0, 0, 2048, "G")
+        coarse(2, 0)
+        denominator(1)
+        coarse(2, 1)
+        ratio(1)
+        by_entity(1)
+        coarse(2, 2)
+        turn(0, 0)
+        turn_copy(0, 0)
+        turn(0, 1)
+        salient(1)
+        nil_share(1)
+        by_mention(1, 0, 2048, "G")
+        turn_copy(0, 1)
+        mention_rows(1, 1)
+        coarse(2, 3)
+        entity_quant(0)
+        mention_rows(1, 2)
+        mention_copy(1, 1)
+        peak(2)
+        mention_copy(1, 2)
+        mention_copy(1, 3)
+        linked(0)
+        logit(3, 0)
+        expo(2)
+        logit(3, 1)
+        turn(1, 0)
+        turn(1, 1)
+        logit(3, 2)
+        score(3, 3)
+        mention_codes(1)
+        turn_copy(1, 0)
+        denominator(2)
+        turn_copy(1, 1)
+        logit(3, 3)
+        score(4, 0)
+        coarse(3, 0)
+        ratio(2)
+        entity_quant(1)
+        salient(2)
+        score(4, 1)
+        nil_share(2)
+        by_mention(2, 0, 2048, "G")
+        coarse(3, 1)
+        linked_out(0)
+        score(4, 2)
+        coarse(3, 2)
+        by_entity(2)
+        coarse(3, 3)
+        linked(1)
+        card_part(5, 3)
+        peak(3)
+        turn(2, 0)
+        turn_copy(2, 0)
+        turn(2, 1)
+        logit(4, 0)
+        expo(3)
+        logit(4, 1)
+        score(4, 3)
+        logit(4, 2)
+        score(5, 0)
+        logit(4, 3)
+        score(5, 1)
+        linked_out(1)
+        turn_copy(2, 1)
+        score(5, 2)
+        denominator(3)
+        logit(5, 0)
+        coarse(4, 0)
+        coarse(4, 1)
+        ratio(3)
+        entity_quant(2)
+        salient(3)
+        nil_share(3)
+        score(5, 3)
+        by_mention(3, 0, 2048, "G")
+        coarse(4, 2)
+        by_entity(3)
+        coarse(4, 3)
+        linked(2)
+        coarse(5, 0)
+        peak(4)
+        turn(3, 0)
+        turn_copy(3, 0)
+        turn(3, 1)
+        logit(5, 1)
+        expo(4)
+        logit(5, 2)
+        score(6, 0)
+        logit(5, 3)
+        score(6, 1)
+        card_codes(5)
+        score(6, 2)
+        linked_out(2)
+        turn_copy(3, 1)
+        denominator(4)
+        coarse(5, 1)
+        logit(6, 0)
+        coarse(5, 2)
+        ratio(4)
+        entity_quant(3)
+        salient(4)
+        nil_share(4)
+        score(6, 3)
+        by_mention(4, 0, 2048, "G")
+        coarse(5, 3)
+        by_entity(4)
+        gather(0, 0, "S")
+        linked(3)
+        gather(0, 1, "S")
+        peak(5)
+        coarse(6, 0)
+        turn(4, 0)
+        turn_copy(4, 0)
+        turn(4, 1)
+        logit(6, 1)
+        expo(5)
+        logit(6, 2)
+        score(7, 0)
+        logit(6, 3)
+        score(7, 1)
+        gather_quant(0, 0)
+        score(7, 2)
+        gather_quant(0, 1)
+        turn_copy(4, 1)
+        denominator(5)
+        linked_out(3)
+        coarse(6, 1)
+        ratio(5)
+        coarse(6, 2)
+        entity_quant(4)
+        salient(5)
+        nil_share(5)
+        by_mention(5, 0, 2048, "G")
+        coarse(6, 3)
+        by_entity(5)
+        gather(0, 2, "S")
+        linked(4)
+        gather(0, 3, "S")
+        peak(6)
+        turn(5, 0)
+        turn_copy(5, 0)
+        turn(5, 1)
+        logit(7, 0)
+        expo(6)
+        logit(7, 1)
+        score(7, 3)
+        logit(7, 2)
+        logit(7, 3)
+        gather_quant(0, 2)
+        turn_copy(5, 1)
+        denominator(6)
+        coarse(7, 0)
+        gather_quant(0, 3)
+        coarse(7, 1)
+        ratio(6)
+        entity_quant(5)
+        salient(6)
+        nil_share(6)
+        by_mention(6, 0, 2048, "G")
+        coarse(7, 2)
+        linked_out(4)
+        coarse(7, 3)
+        by_entity(6)
+        linked(5)
+        peak(7)
+        turn(6, 0)
+        turn_copy(6, 0)
+        turn(6, 1)
+        linked_out(5)
+        expo(7)
+        turn_copy(6, 1)
+        denominator(7)
+        ratio(7)
+        salient(7)
+        by_entity(7)
+        nil_share(7)
+        by_mention(7, 0, 512, "G")
+        by_mention(7, 1, 512, "S")
+        by_mention(7, 3, 512, "S")
+        by_mention(7, 2, 512, "G")
+        gather(1, 1, "S")
+        entity_quant(6)
+        turn(7, 0)
+        gather(1, 0, "V")
+        turn_copy(7, 0)
+        gather(1, 2, "V")
+        linked(6)
+        gather_quant(1, 0)
+        linked_out(6)
+        turn(7, 1)
+        profile(0, "sc")
+        turn_copy(7, 1)
+        profile(1, "acc")
+        gather_quant(1, 1)
+        profile(2, "sc")
+        profile_out(0, "S")
+        gather(1, 3, "V")
+        profile(3, "acc")
+        profile_out(2, "S")
+        profile(4, "sc")
+        gather_quant(1, 2)
+        profile_out(4, "S")
+        profile(5, "sc")
+        gather_quant(1, 3)
+        profile(7, "sc")
+        profile_out(1, "V")
+        profile(9, "sc")
+        entity_quant(7)
+        profile(6, "acc")
+        profile_out(3, "V")
+        profile_out(6, "S")
+        profile_out(5, "V")
+        profile(8, "acc")
+        profile_out(7, "V")
+        profile_out(8, "S")
+        profile(10, "sc")
+        profile_out(9, "V")
+        profile(11, "acc")
+        profile_out(10, "S")
+        profile_out(11, "V")
+        profile(12, "sc")
+        profile(13, "acc")
+        profile_out(12, "S")
+        profile_out(13, "V")
+        linked(7)
+        linked_out(7)
+        profile(14, "sc")
+        profile_out(14, "S")
+        profile(15, "sc")
+        profile_out(15, "V")

@@ -111,12 +111,12 @@ def tile_entity_linking_lift_f6_kernel(
         def copy_rows(xt, grouped):
             nc.scalar.copy(out=grouped, in_=xt[:].rearrange("p c u r -> p c r u"))
 
-        mgs, mq, mqs = [], [], []
+        mgs, mq, mqs = {}, {}, {}
 
         def mention_rows(g, t):
-            if t == 0:
+            if g not in mgs:
                 mg = work.tile([P, 4, KP, P, 4], BF16, tag="big", bufs=4, align_bytes=64)
-                mgs.append(mg)
+                mgs[g] = mg
             grouped = mgs[g][:, t].rearrange("p c r j -> p (c r j)").bitcast(F32).rearrange("p (c r u) -> p c r u", c=KP, u=2)
             S["mt", g, t] = transpose_rows(mraws[g][:, t, :]), grouped
 
@@ -127,15 +127,14 @@ def tile_entity_linking_lift_f6_kernel(
             codes = keep.tile([P, 4 * KP * P], U32, tag="mq", bufs=2, align_bytes=64)
             scales = keep.tile([P, 4 * KP * P], U8, tag="mqs", bufs=2, align_bytes=64)
             quantize(nc, codes[:], scales[:], mgs[g][:].rearrange("p t c r j -> p (t c r j)"))
-            mq.append(codes)
-            mqs.append(scales)
+            mq[g], mqs[g] = codes, scales
 
-        egs, xbs, eq, eqs = [], {}, [], []
+        egs, xbs, eq, eqs = {}, {}, {}, {}
 
         def entity_scale(c, q):
-            if q == 0:
+            if c not in egs:
                 eg = work.tile([P, KP, 4, P, 4], BF16, tag="big", bufs=4, align_bytes=64)
-                egs.append(eg)
+                egs[c] = eg
             xb = work.tile([P, K], BF16, tag="xb", bufs=3)
             nc.vector.tensor_tensor(out=xb[:], in0=ebytes[c][:, q, :].bitcast(FP8), in1=scale_b[:], op=ALU.mult)
             xbs[c, q] = xb
@@ -151,15 +150,14 @@ def tile_entity_linking_lift_f6_kernel(
             codes = keep.tile([P, KP * 512], U32, tag="eq", bufs=4, align_bytes=64)
             scales = keep.tile([P, KP * 512], U8, tag="eqs", bufs=4, align_bytes=64)
             quantize(nc, codes[:], scales[:], egs[c][:].rearrange("p c q r j -> p (c q r j)"))
-            eq.append(codes)
-            eqs.append(scales)
+            eq[c], eqs[c] = codes, scales
 
-        cgs, cq, cqs = [], [], []
+        cgs, cq, cqs = {}, {}, {}
 
         def card_part(g, part):
-            if part == 0:
+            if g not in cgs:
                 cg = work.tile([P, D, 4], BF16, tag="grp", bufs=4, align_bytes=64)
-                cgs.append(cg)
+                cgs[g] = cg
             cols = slice(part * 128, (part + 1) * 128)
             nc.scalar.copy(out=cgs[g][:, cols, :], in_=craws[g][:, :, cols].rearrange("p t d -> p d t"))
 
@@ -167,8 +165,7 @@ def tile_entity_linking_lift_f6_kernel(
             codes = keep.tile([P, D], U32, tag="cq", bufs=6, align_bytes=64)
             scales = keep.tile([P, D], U8, tag="cqs", bufs=6, align_bytes=64)
             quantize(nc, codes[:], scales[:], cgs[g][:].rearrange("p d j -> p (d j)"))
-            cq.append(codes)
-            cqs.append(scales)
+            cq[g], cqs[g] = codes, scales
 
         bmq, bmqs, bmp = [], [], []
         for g in range(G_M):
@@ -193,7 +190,7 @@ def tile_entity_linking_lift_f6_kernel(
             S["sc", i, c] = sc
 
         def logit(i, c):
-            if c == 0:
+            if ("z", i) not in S:
                 z = work.tile([P, E], F32, tag="z", bufs=3)
                 zb = work.tile([P, E], BF16, tag="zb", bufs=2)
                 S["z", i], S["zb", i] = z, zb
@@ -243,8 +240,10 @@ def tile_entity_linking_lift_f6_kernel(
             dst = bmp[g][:, t // 2, cols, t % 2]
             if eng == "G":
                 nc.gpsimd.tensor_scalar(out=dst, in0=z[:, cols], scalar1=fsal[:], scalar2=0.0, op0=ALU.mult, op1=ALU.add)
-            else:
+            elif eng == "S":
                 nc.scalar.activation(out=dst, in_=z[:, cols], func=ACT.Copy, scale=fsal[:])
+            else:
+                nc.vector.tensor_scalar(out=dst, in0=z[:, cols], scalar1=fsal[:], scalar2=None, op0=ALU.mult)
 
         def nil_share(i):
             pnil = small.tile([P, 1], F32)
@@ -259,7 +258,7 @@ def tile_entity_linking_lift_f6_kernel(
             S["be", i] = be
 
         def turn(i, h):
-            if h == 0:
+            if ("bg", i) not in S:
                 bg = work.tile([P, G_E, P, 4], BF16, tag="grp", bufs=4, align_bytes=64)
                 S["bg", i] = bg
             words = S["be", i][:].bitcast(F32)
@@ -326,7 +325,7 @@ def tile_entity_linking_lift_f6_kernel(
             S["prof", r] = acc
 
         def profile_out(r, eng):
-            if r % 4 == 0:
+            if ("wide", r // 4) not in S:
                 wide = work.tile([P, 4, D], F32, tag="z", bufs=3)
                 S["wide", r // 4] = wide
             res = S["wide", r // 4][:, r % 4, :]
@@ -337,369 +336,369 @@ def tile_entity_linking_lift_f6_kernel(
             nc.sync.dma_start(out=out_1[r * P : (r + 1) * P, :], in_=res)
 
         entity_scale(0, 0)
-        entity_scale(0, 1)
+        entity_scale(0, 2)
         entity_rows(0, 0)
         entity_copy(0, 0)
-        entity_scale(0, 2)
-        entity_rows(0, 1)
-        entity_copy(0, 1)
         entity_scale(0, 3)
+        entity_rows(0, 2)
+        entity_copy(0, 2)
+        entity_scale(0, 1)
         mention_rows(0, 0)
         mention_copy(0, 0)
         mention_rows(0, 1)
-        mention_copy(0, 1)
-        entity_rows(0, 2)
-        entity_scale(1, 0)
-        entity_copy(0, 2)
-        mention_rows(0, 2)
-        mention_copy(0, 2)
-        entity_rows(0, 3)
-        entity_scale(1, 1)
-        entity_copy(0, 3)
-        mention_rows(0, 3)
-        mention_copy(0, 3)
-        entity_rows(1, 0)
-        entity_codes(0)
-        entity_copy(1, 0)
-        entity_rows(1, 1)
-        entity_copy(1, 1)
-        mention_codes(0)
-        card_part(0, 0)
-        entity_scale(1, 2)
-        card_part(0, 1)
-        score(0, 0)
-        card_part(0, 2)
-        score(1, 0)
         entity_scale(1, 3)
-        card_part(0, 3)
-        entity_rows(1, 2)
-        card_part(1, 0)
-        logit(0, 0)
-        entity_copy(1, 2)
+        entity_scale(1, 1)
+        mention_rows(0, 2)
+        entity_scale(1, 0)
+        mention_copy(0, 1)
+        entity_rows(0, 3)
+        entity_scale(1, 2)
+        mention_rows(0, 3)
         entity_rows(1, 3)
-        logit(1, 0)
-        entity_copy(1, 3)
-        entity_scale(2, 0)
-        coarse(0, 0)
-        coarse(1, 0)
-        entity_codes(1)
-        card_part(1, 1)
-        entity_rows(2, 0)
-        entity_copy(2, 0)
-        entity_scale(2, 1)
-        card_part(1, 2)
-        score(0, 1)
-        score(1, 1)
-        card_part(1, 3)
-        card_codes(0)
-        card_part(2, 0)
         entity_scale(2, 2)
-        entity_rows(2, 1)
-        entity_copy(2, 1)
-        logit(0, 1)
-        card_part(2, 1)
-        entity_rows(2, 2)
-        logit(1, 1)
-        card_part(2, 2)
-        entity_scale(2, 3)
-        entity_copy(2, 2)
-        coarse(0, 1)
-        entity_scale(3, 0)
-        coarse(1, 1)
-        entity_rows(2, 3)
-        entity_copy(2, 3)
-        card_codes(1)
-        card_part(2, 3)
-        entity_rows(3, 0)
-        entity_codes(2)
-        entity_copy(3, 0)
-        card_part(3, 0)
+        entity_rows(0, 1)
+        entity_rows(1, 1)
+        mention_copy(0, 2)
+        entity_copy(0, 3)
         entity_scale(3, 1)
-        card_part(3, 1)
-        score(0, 2)
-        card_part(3, 2)
-        score(1, 2)
-        entity_scale(3, 2)
-        card_part(3, 3)
+        mention_copy(0, 3)
+        entity_scale(2, 3)
+        entity_copy(1, 3)
+        entity_copy(0, 1)
+        entity_copy(1, 1)
+        entity_rows(1, 2)
+        card_part(0, 0)
+        entity_rows(1, 0)
+        card_part(0, 2)
         entity_rows(3, 1)
+        card_part(0, 3)
+        card_part(0, 1)
+        card_part(2, 1)
+        card_part(2, 3)
+        mention_codes(0)
+        entity_scale(3, 0)
+        entity_copy(1, 2)
+        card_part(1, 2)
+        entity_copy(1, 0)
+        card_part(2, 0)
+        entity_codes(1)
+        entity_rows(3, 0)
+        card_part(1, 0)
+        card_part(2, 2)
+        entity_copy(3, 0)
+        entity_rows(2, 3)
+        entity_codes(0)
         entity_copy(3, 1)
-        entity_scale(3, 3)
+        entity_scale(3, 2)
+        score(1, 1)
+        card_part(3, 2)
+        card_part(3, 0)
+        score(0, 1)
+        entity_rows(2, 2)
+        entity_copy(2, 3)
+        score(1, 0)
         entity_rows(3, 2)
-        card_part(4, 0)
+        entity_scale(2, 1)
+        card_part(1, 1)
+        entity_scale(2, 0)
+        entity_copy(2, 2)
+        card_part(3, 3)
+        entity_scale(3, 3)
         card_codes(2)
-        entity_copy(3, 2)
+        card_part(3, 1)
+        logit(1, 0)
+        entity_rows(2, 1)
+        logit(0, 1)
+        entity_rows(2, 0)
+        mention_rows(1, 2)
         entity_rows(3, 3)
-        logit(0, 2)
-        card_part(4, 1)
-        logit(1, 2)
-        entity_copy(3, 3)
-        card_codes(3)
-        coarse(0, 2)
-        score(2, 0)
-        entity_codes(3)
-        coarse(1, 2)
-        card_part(4, 2)
+        score(0, 0)
+        card_codes(0)
+        entity_copy(2, 0)
+        entity_copy(2, 1)
         mention_rows(1, 0)
-        logit(2, 0)
-        mention_copy(1, 0)
-        score(0, 3)
+        mention_rows(1, 1)
+        entity_copy(3, 2)
+        mention_copy(1, 2)
+        entity_copy(3, 3)
+        logit(1, 1)
         card_part(4, 3)
-        logit(0, 3)
-        score(1, 3)
-        card_part(5, 0)
-        logit(1, 3)
-        score(2, 3)
-        coarse(0, 3)
-        logit(2, 3)
-        score(2, 1)
-        coarse(1, 3)
-        score(2, 2)
-        peak(0)
-        card_part(5, 1)
-        score(3, 2)
-        card_part(5, 2)
-        peak(1)
+        entity_codes(2)
+        entity_codes(3)
+        score(0, 2)
+        mention_copy(1, 0)
+        coarse(1, 0)
+        coarse(0, 1)
         mention_rows(1, 3)
-        expo(0)
+        logit(0, 2)
+        coarse(1, 1)
+        score(0, 3)
+        logit(0, 0)
+        score(2, 1)
+        score(1, 3)
+        logit(0, 3)
         logit(2, 1)
-        logit(2, 2)
-        score(3, 0)
-        card_codes(4)
-        expo(1)
+        mention_copy(1, 3)
+        score(1, 2)
+        coarse(0, 2)
+        logit(1, 3)
+        coarse(0, 0)
+        coarse(0, 3)
+        card_part(5, 2)
+        score(2, 3)
+        score(3, 2)
+        logit(1, 2)
+        score(2, 2)
         score(3, 1)
+        score(2, 0)
+        peak(0)
+        coarse(1, 3)
+        coarse(1, 2)
+        logit(2, 3)
+        peak(1)
+        mention_copy(1, 1)
+        logit(2, 2)
+        card_codes(3)
+        expo(0)
+        expo(1)
+        score(3, 0)
         denominator(0)
         ratio(0)
-        salient(0)
-        by_entity(0)
-        nil_share(0)
-        by_mention(0, 0, 2048, "G")
-        coarse(2, 0)
-        denominator(1)
         coarse(2, 1)
-        ratio(1)
-        by_entity(1)
+        mention_codes(1)
+        by_entity(0)
+        logit(2, 0)
         coarse(2, 2)
-        turn(0, 0)
-        turn_copy(0, 0)
-        turn(0, 1)
-        salient(1)
-        nil_share(1)
-        by_mention(1, 0, 2048, "G")
-        turn_copy(0, 1)
-        mention_rows(1, 1)
-        coarse(2, 3)
-        entity_quant(0)
-        mention_rows(1, 2)
-        mention_copy(1, 1)
-        peak(2)
-        mention_copy(1, 2)
-        mention_copy(1, 3)
-        linked(0)
-        logit(3, 0)
-        expo(2)
+        card_part(5, 3)
+        denominator(1)
+        salient(0)
+        ratio(1)
+        score(3, 3)
+        card_part(4, 2)
         logit(3, 1)
+        turn(0, 1)
+        coarse(2, 3)
+        coarse(2, 0)
+        logit(3, 0)
+        card_part(1, 3)
+        score(4, 1)
+        peak(2)
+        card_part(4, 1)
+        score(4, 0)
+        turn(0, 0)
+        by_mention(0, 0, 2048, "G")
+        salient(1)
+        logit(3, 3)
+        card_part(4, 0)
+        logit(3, 2)
+        by_mention(1, 0, 2048, "G")
+        expo(2)
+        score(4, 2)
+        by_entity(1)
         turn(1, 0)
         turn(1, 1)
-        logit(3, 2)
-        score(3, 3)
-        mention_codes(1)
-        turn_copy(1, 0)
-        denominator(2)
-        turn_copy(1, 1)
-        logit(3, 3)
-        score(4, 0)
-        coarse(3, 0)
-        ratio(2)
-        entity_quant(1)
-        salient(2)
-        score(4, 1)
-        nil_share(2)
-        by_mention(2, 0, 2048, "G")
-        coarse(3, 1)
-        linked_out(0)
-        score(4, 2)
+        turn_copy(0, 1)
         coarse(3, 2)
-        by_entity(2)
+        denominator(2)
         coarse(3, 3)
-        linked(1)
-        card_part(5, 3)
-        peak(3)
-        turn(2, 0)
-        turn_copy(2, 0)
-        turn(2, 1)
-        logit(4, 0)
-        expo(3)
-        logit(4, 1)
-        score(4, 3)
-        logit(4, 2)
-        score(5, 0)
-        logit(4, 3)
-        score(5, 1)
-        linked_out(1)
-        turn_copy(2, 1)
-        score(5, 2)
-        denominator(3)
-        logit(5, 0)
-        coarse(4, 0)
-        coarse(4, 1)
-        ratio(3)
-        entity_quant(2)
-        salient(3)
-        nil_share(3)
-        score(5, 3)
-        by_mention(3, 0, 2048, "G")
-        coarse(4, 2)
-        by_entity(3)
-        coarse(4, 3)
-        linked(2)
-        coarse(5, 0)
-        peak(4)
-        turn(3, 0)
-        turn_copy(3, 0)
-        turn(3, 1)
-        logit(5, 1)
-        expo(4)
-        logit(5, 2)
-        score(6, 0)
-        logit(5, 3)
-        score(6, 1)
-        card_codes(5)
-        score(6, 2)
-        linked_out(2)
-        turn_copy(3, 1)
-        denominator(4)
-        coarse(5, 1)
-        logit(6, 0)
-        coarse(5, 2)
-        ratio(4)
-        entity_quant(3)
-        salient(4)
-        nil_share(4)
+        coarse(3, 1)
+        card_codes(4)
+        ratio(2)
+        coarse(3, 0)
         score(6, 3)
-        by_mention(4, 0, 2048, "G")
-        coarse(5, 3)
-        by_entity(4)
-        gather(0, 0, "S")
-        linked(3)
-        gather(0, 1, "S")
-        peak(5)
-        coarse(6, 0)
-        turn(4, 0)
-        turn_copy(4, 0)
-        turn(4, 1)
+        logit(4, 2)
+        logit(4, 0)
+        logit(4, 1)
+        coarse(4, 2)
+        score(6, 0)
+        salient(2)
+        peak(3)
+        card_part(5, 0)
+        score(4, 3)
+        coarse(4, 1)
+        logit(4, 3)
+        by_mention(2, 0, 2048, "G")
+        by_entity(2)
+        score(6, 1)
+        expo(3)
+        card_part(5, 1)
+        turn_copy(0, 0)
+        score(6, 2)
+        coarse(4, 0)
+        denominator(3)
+        nil_share(0)
+        score(5, 0)
+        card_codes(1)
+        ratio(3)
         logit(6, 1)
-        expo(5)
-        logit(6, 2)
-        score(7, 0)
+        coarse(4, 3)
         logit(6, 3)
-        score(7, 1)
-        gather_quant(0, 0)
-        score(7, 2)
-        gather_quant(0, 1)
-        turn_copy(4, 1)
-        denominator(5)
-        linked_out(3)
-        coarse(6, 1)
-        ratio(5)
-        coarse(6, 2)
-        entity_quant(4)
-        salient(5)
-        nil_share(5)
-        by_mention(5, 0, 2048, "G")
+        turn_copy(1, 0)
+        logit(6, 0)
+        salient(3)
+        peak(4)
         coarse(6, 3)
-        by_entity(5)
-        gather(0, 2, "S")
-        linked(4)
+        logit(6, 2)
+        coarse(6, 1)
+        score(5, 2)
+        score(5, 1)
+        entity_quant(0)
+        score(5, 3)
+        linked(0)
+        expo(4)
+        score(7, 2)
+        by_mention(3, 0, 2048, "G")
         gather(0, 3, "S")
-        peak(6)
-        turn(5, 0)
-        turn_copy(5, 0)
-        turn(5, 1)
-        logit(7, 0)
-        expo(6)
-        logit(7, 1)
-        score(7, 3)
-        logit(7, 2)
-        logit(7, 3)
+        turn_copy(1, 1)
+        by_entity(3)
+        turn(2, 1)
+        turn(2, 0)
+        logit(5, 1)
+        card_codes(5)
+        gather(0, 2, "S")
+        gather(0, 1, "S")
+        gather(0, 0, "S")
+        denominator(4)
+        logit(5, 2)
+        ratio(4)
         gather_quant(0, 2)
-        turn_copy(5, 1)
-        denominator(6)
-        coarse(7, 0)
-        gather_quant(0, 3)
-        coarse(7, 1)
-        ratio(6)
-        entity_quant(5)
-        salient(6)
-        nil_share(6)
-        by_mention(6, 0, 2048, "G")
-        coarse(7, 2)
-        linked_out(4)
+        logit(5, 3)
+        logit(5, 0)
+        gather_quant(0, 1)
+        coarse(5, 3)
+        score(7, 1)
+        by_entity(4)
+        salient(4)
+        score(7, 3)
+        coarse(5, 0)
+        coarse(5, 2)
+        coarse(5, 1)
+        peak(5)
+        nil_share(3)
+        coarse(6, 2)
+        coarse(6, 0)
+        turn(3, 0)
+        logit(7, 3)
+        by_mention(4, 0, 2048, "G")
+        turn_copy(2, 1)
+        expo(5)
+        peak(6)
+        logit(7, 1)
+        denominator(5)
         coarse(7, 3)
-        by_entity(6)
-        linked(5)
+        ratio(5)
+        entity_quant(1)
+        nil_share(4)
+        turn(3, 1)
+        score(7, 0)
+        turn(4, 0)
+        by_entity(5)
+        nil_share(1)
+        expo(6)
+        logit(7, 0)
+        turn_copy(3, 1)
+        coarse(7, 1)
+        logit(7, 2)
+        denominator(6)
+        turn_copy(3, 0)
+        turn(4, 1)
+        ratio(6)
+        gather_quant(0, 3)
+        linked(1)
+        coarse(7, 0)
+        salient(5)
+        entity_quant(3)
+        coarse(7, 2)
         peak(7)
-        turn(6, 0)
-        turn_copy(6, 0)
-        turn(6, 1)
-        linked_out(5)
+        by_mention(5, 0, 2048, "G")
+        linked_out(1)
+        linked_out(0)
+        turn_copy(4, 0)
+        turn(5, 1)
+        turn_copy(4, 1)
+        turn(5, 0)
+        linked(3)
+        entity_quant(4)
+        turn_copy(2, 0)
         expo(7)
-        turn_copy(6, 1)
+        entity_quant(2)
+        salient(6)
         denominator(7)
         ratio(7)
+        turn_copy(5, 1)
+        turn_copy(5, 0)
+        by_mention(6, 0, 2048, "G")
+        by_entity(6)
         salient(7)
-        by_entity(7)
-        nil_share(7)
-        by_mention(7, 0, 512, "G")
-        by_mention(7, 1, 512, "S")
-        by_mention(7, 3, 512, "S")
-        by_mention(7, 2, 512, "G")
-        gather(1, 1, "S")
-        entity_quant(6)
-        turn(7, 0)
-        gather(1, 0, "V")
-        turn_copy(7, 0)
-        gather(1, 2, "V")
-        linked(6)
-        gather_quant(1, 0)
-        linked_out(6)
-        turn(7, 1)
-        profile(0, "sc")
-        turn_copy(7, 1)
-        profile(1, "acc")
-        gather_quant(1, 1)
-        profile(2, "sc")
-        profile_out(0, "S")
-        gather(1, 3, "V")
-        profile(3, "acc")
-        profile_out(2, "S")
-        profile(4, "sc")
-        gather_quant(1, 2)
-        profile_out(4, "S")
-        profile(5, "sc")
+        by_mention(7, 2, 512, "S")
+        by_mention(7, 3, 512, "G")
+        entity_quant(5)
+        nil_share(2)
+        gather(1, 3, "S")
         gather_quant(1, 3)
+        nil_share(5)
+        linked(2)
+        by_mention(7, 1, 512, "G")
+        turn(6, 1)
+        linked_out(3)
+        gather(1, 1, "S")
+        gather_quant(1, 1)
+        turn(6, 0)
+        profile(12, "sc")
+        gather(1, 2, "S")
+        linked_out(2)
+        gather_quant(1, 2)
+        profile(15, "sc")
+        profile(13, "acc")
+        gather_quant(0, 0)
+        profile_out(15, "S")
+        profile(4, "sc")
+        by_entity(7)
         profile(7, "sc")
-        profile_out(1, "V")
-        profile(9, "sc")
-        entity_quant(7)
-        profile(6, "acc")
-        profile_out(3, "V")
-        profile_out(6, "S")
-        profile_out(5, "V")
+        profile_out(13, "S")
+        turn_copy(6, 1)
+        profile_out(4, "S")
+        profile_out(7, "S")
+        profile(11, "acc")
+        linked(4)
+        profile_out(12, "S")
+        profile(14, "sc")
+        nil_share(6)
+        by_mention(7, 0, 512, "V")
+        linked_out(4)
+        profile(5, "sc")
+        turn_copy(6, 0)
+        profile_out(14, "S")
+        turn(7, 0)
+        profile_out(11, "S")
+        gather(1, 0, "S")
+        turn(7, 1)
+        gather_quant(1, 0)
         profile(8, "acc")
-        profile_out(7, "V")
         profile_out(8, "S")
         profile(10, "sc")
-        profile_out(9, "V")
-        profile(11, "acc")
+        turn_copy(7, 0)
+        linked(5)
+        profile(1, "acc")
+        linked_out(5)
+        nil_share(7)
         profile_out(10, "S")
-        profile_out(11, "V")
-        profile(12, "sc")
-        profile(13, "acc")
-        profile_out(12, "S")
-        profile_out(13, "V")
+        turn_copy(7, 1)
+        profile(9, "sc")
+        entity_quant(7)
+        profile(3, "acc")
+        profile_out(1, "S")
+        entity_quant(6)
+        profile(0, "sc")
+        profile_out(5, "S")
+        profile_out(3, "S")
+        profile_out(0, "S")
         linked(7)
         linked_out(7)
-        profile(14, "sc")
-        profile_out(14, "S")
-        profile(15, "sc")
-        profile_out(15, "V")
+        linked(6)
+        profile_out(9, "S")
+        profile(2, "sc")
+        profile_out(2, "S")
+        profile(6, "acc")
+        profile_out(6, "S")
+        linked_out(6)

@@ -43,7 +43,7 @@ def tile_entity_linking_lift_f6_kernel(
         sharp_h = const.tile([P, G_M, 4], BF16)
         nil_h = const.tile([P, G_M, 4], BF16)
         sal_h = const.tile([P, G_M, 4], BF16)
-        nc.scalar.dma_start(out=scale_b[:], in_=entities_scale.rearrange("o k -> (o k)").partition_broadcast(P))
+        nc.sync.dma_start(out=scale_b[:], in_=entities_scale.rearrange("o k -> (o k)").partition_broadcast(P))
         warm = const.tile([P, 1], F32)
         nc.vector.memset(warm[:], 0.0)
         nc.scalar.activation(out=warm[:], in_=warm[:], func=ACT.Exp)
@@ -75,9 +75,9 @@ def tile_entity_linking_lift_f6_kernel(
         nc.gpsimd.dma_start(out=sharp_h[:], in_=sharpness.rearrange("(g p t) -> p g t", p=P, t=4))
         nc.gpsimd.dma_start(out=nil_h[:], in_=nil.rearrange("(g p t) -> p g t", p=P, t=4))
         nc.gpsimd.dma_start(out=sal_h[:], in_=salience.rearrange("(g p t) -> p g t", p=P, t=4))
-        nc.sync.dma_start(out=prior_b[:], in_=prior.partition_broadcast(P))
         load_entities(2, 0, 4)
         load_entities(3, 0, 4)
+        nc.sync.dma_start(out=prior_b[:], in_=prior.partition_broadcast(P))
 
         sharp = const.tile([P, G_M * 4], F32)
         nilv = const.tile([P, G_M * 4], F32)
@@ -159,7 +159,10 @@ def tile_entity_linking_lift_f6_kernel(
                 cg = work.tile([P, D, 4], BF16, tag="grp", bufs=4, align_bytes=64)
                 cgs[g] = cg
             cols = slice(part * 128, (part + 1) * 128)
-            nc.scalar.copy(out=cgs[g][:, cols, :], in_=craws[g][:, :, cols].rearrange("p t d -> p d t"))
+            nc.scalar.copy(
+                out=cgs[g][:, cols, :].rearrange("p (c i) t -> p c t i", i=4),
+                in_=craws[g][:, :, cols].rearrange("p t (c i) -> p c t i", i=4),
+            )
 
         def card_codes(g):
             codes = keep.tile([P, D], U32, tag="cq", bufs=6, align_bytes=64)
@@ -173,8 +176,8 @@ def tile_entity_linking_lift_f6_kernel(
             scales = keep.tile([P, E], U8, tag="bmqs", bufs=2, align_bytes=64)
             bmq.append(codes)
             bmqs.append(scales)
-            pairs = work.tile([P, 2, E, 2], BF16, tag="bmp", bufs=1)
-            bmp.append(pairs)
+            planes = work.tile([P, 4, E], BF16, tag="bmp", bufs=1)
+            bmp.append(planes)
 
         def score(i, c):
             g, t = divmod(i, 4)
@@ -237,7 +240,7 @@ def tile_entity_linking_lift_f6_kernel(
             g, t = divmod(i, 4)
             z, fsal = S["z", i], S["fsal", i]
             cols = slice(j * n, (j + 1) * n)
-            dst = bmp[g][:, t // 2, cols, t % 2]
+            dst = bmp[g][:, t, cols]
             if eng == "G":
                 nc.gpsimd.tensor_scalar(out=dst, in0=z[:, cols], scalar1=fsal[:], scalar2=0.0, op0=ALU.mult, op1=ALU.add)
             elif eng == "S":
@@ -300,8 +303,8 @@ def tile_entity_linking_lift_f6_kernel(
 
         def gather(g, c, eng):
             bmi = work.tile([P, 512, 4], BF16, tag="grp", bufs=4, align_bytes=64)
-            src = bmp[g][:, :, c * 512 : (c + 1) * 512, :].rearrange("p u e v -> p u (e v)").bitcast(F32).rearrange("p u e -> p e u")
-            dst = bmi[:].rearrange("p e j -> p (e j)").bitcast(F32).rearrange("p (e u) -> p e u", u=2)
+            src = bmp[g][:, :, c * 512 : (c + 1) * 512].rearrange("p t (q i) -> p q t i", i=4)
+            dst = bmi[:].rearrange("p (q i) t -> p q t i", i=4)
             if eng == "V":
                 nc.vector.tensor_copy(out=dst, in_=src)
             else:
@@ -336,369 +339,369 @@ def tile_entity_linking_lift_f6_kernel(
             nc.sync.dma_start(out=out_1[r * P : (r + 1) * P, :], in_=res)
 
         entity_scale(0, 0)
-        entity_scale(0, 2)
-        entity_rows(0, 0)
-        entity_copy(0, 0)
-        entity_scale(0, 3)
-        entity_rows(0, 2)
-        entity_copy(0, 2)
         entity_scale(0, 1)
+        entity_rows(0, 0)
+        entity_scale(0, 2)
+        entity_rows(0, 1)
         mention_rows(0, 0)
+        entity_scale(0, 3)
+        entity_copy(0, 0)
+        entity_rows(0, 2)
         mention_copy(0, 0)
         mention_rows(0, 1)
-        entity_scale(1, 3)
-        entity_scale(1, 1)
-        mention_rows(0, 2)
-        entity_scale(1, 0)
-        mention_copy(0, 1)
         entity_rows(0, 3)
-        entity_scale(1, 2)
+        entity_scale(1, 0)
         mention_rows(0, 3)
-        entity_rows(1, 3)
-        entity_scale(2, 2)
-        entity_rows(0, 1)
-        entity_rows(1, 1)
-        mention_copy(0, 2)
-        entity_copy(0, 3)
-        entity_scale(3, 1)
-        mention_copy(0, 3)
-        entity_scale(2, 3)
-        entity_copy(1, 3)
+        entity_copy(0, 2)
+        mention_rows(0, 2)
         entity_copy(0, 1)
-        entity_copy(1, 1)
-        entity_rows(1, 2)
-        card_part(0, 0)
+        entity_scale(1, 2)
+        entity_scale(1, 3)
         entity_rows(1, 0)
+        mention_copy(0, 1)
+        entity_rows(1, 3)
+        entity_scale(1, 1)
+        entity_rows(1, 2)
+        entity_scale(2, 2)
+        mention_copy(0, 3)
+        entity_copy(1, 0)
+        entity_scale(3, 3)
+        entity_scale(2, 1)
+        entity_copy(0, 3)
+        entity_codes(0)
+        mention_copy(0, 2)
+        entity_copy(1, 2)
+        entity_scale(3, 2)
+        mention_codes(0)
+        entity_rows(1, 1)
+        entity_scale(2, 0)
+        entity_rows(2, 2)
+        card_part(0, 3)
+        card_part(0, 0)
+        entity_copy(1, 3)
+        card_part(1, 0)
+        entity_rows(3, 3)
+        card_part(1, 3)
+        entity_copy(1, 1)
+        entity_scale(2, 3)
+        card_part(0, 1)
+        entity_rows(2, 1)
+        card_part(2, 3)
+        entity_rows(3, 2)
+        entity_copy(2, 1)
+        entity_scale(3, 0)
+        score(0, 0)
+        card_part(2, 1)
+        entity_scale(3, 1)
+        entity_rows(2, 0)
+        entity_rows(2, 3)
+        score(1, 0)
+        logit(0, 0)
+        entity_copy(3, 3)
+        entity_copy(3, 2)
+        entity_rows(3, 0)
+        mention_rows(1, 1)
+        entity_codes(1)
         card_part(0, 2)
         entity_rows(3, 1)
-        card_part(0, 3)
-        card_part(0, 1)
-        card_part(2, 1)
-        card_part(2, 3)
-        mention_codes(0)
-        entity_scale(3, 0)
-        entity_copy(1, 2)
-        card_part(1, 2)
-        entity_copy(1, 0)
-        card_part(2, 0)
-        entity_codes(1)
-        entity_rows(3, 0)
-        card_part(1, 0)
-        card_part(2, 2)
-        entity_copy(3, 0)
-        entity_rows(2, 3)
-        entity_codes(0)
-        entity_copy(3, 1)
-        entity_scale(3, 2)
-        score(1, 1)
-        card_part(3, 2)
-        card_part(3, 0)
         score(0, 1)
-        entity_rows(2, 2)
-        entity_copy(2, 3)
-        score(1, 0)
-        entity_rows(3, 2)
-        entity_scale(2, 1)
-        card_part(1, 1)
-        entity_scale(2, 0)
-        entity_copy(2, 2)
-        card_part(3, 3)
-        entity_scale(3, 3)
-        card_codes(2)
-        card_part(3, 1)
-        logit(1, 0)
-        entity_rows(2, 1)
-        logit(0, 1)
-        entity_rows(2, 0)
-        mention_rows(1, 2)
-        entity_rows(3, 3)
-        score(0, 0)
-        card_codes(0)
-        entity_copy(2, 0)
-        entity_copy(2, 1)
-        mention_rows(1, 0)
-        mention_rows(1, 1)
-        entity_copy(3, 2)
-        mention_copy(1, 2)
-        entity_copy(3, 3)
-        logit(1, 1)
-        card_part(4, 3)
-        entity_codes(2)
-        entity_codes(3)
-        score(0, 2)
-        mention_copy(1, 0)
-        coarse(1, 0)
-        coarse(0, 1)
         mention_rows(1, 3)
+        entity_copy(2, 2)
+        entity_copy(2, 3)
+        card_part(1, 1)
+        entity_copy(2, 0)
+        entity_copy(3, 0)
+        entity_codes(2)
+        score(1, 1)
+        logit(0, 1)
+        card_part(2, 0)
+        logit(1, 0)
+        score(0, 2)
+        entity_copy(3, 1)
+        entity_codes(3)
+        card_part(3, 1)
+        mention_copy(1, 1)
         logit(0, 2)
-        coarse(1, 1)
-        score(0, 3)
-        logit(0, 0)
-        score(2, 1)
-        score(1, 3)
-        logit(0, 3)
-        logit(2, 1)
-        mention_copy(1, 3)
-        score(1, 2)
-        coarse(0, 2)
-        logit(1, 3)
+        mention_rows(1, 2)
+        card_codes(0)
+        mention_rows(1, 0)
         coarse(0, 0)
-        coarse(0, 3)
-        card_part(5, 2)
-        score(2, 3)
-        score(3, 2)
-        logit(1, 2)
+        score(0, 3)
+        score(1, 3)
+        score(1, 2)
+        logit(0, 3)
+        logit(1, 1)
+        logit(1, 3)
         score(2, 2)
-        score(3, 1)
+        coarse(0, 1)
+        mention_copy(1, 3)
+        score(2, 3)
+        coarse(1, 0)
+        card_part(1, 2)
+        logit(1, 2)
+        mention_copy(1, 2)
+        logit(2, 2)
+        card_part(3, 3)
         score(2, 0)
+        score(2, 1)
+        coarse(0, 3)
+        mention_copy(1, 0)
+        coarse(0, 2)
+        score(3, 1)
+        coarse(1, 2)
         peak(0)
         coarse(1, 3)
-        coarse(1, 2)
-        logit(2, 3)
-        peak(1)
-        mention_copy(1, 1)
-        logit(2, 2)
-        card_codes(3)
-        expo(0)
-        expo(1)
         score(3, 0)
+        logit(2, 0)
+        logit(2, 3)
+        coarse(1, 1)
+        expo(0)
+        card_codes(1)
+        card_part(3, 2)
+        peak(1)
         denominator(0)
+        coarse(2, 2)
+        score(3, 2)
+        logit(2, 1)
+        expo(1)
+        coarse(2, 3)
         ratio(0)
-        coarse(2, 1)
         mention_codes(1)
         by_entity(0)
-        logit(2, 0)
-        coarse(2, 2)
-        card_part(5, 3)
         denominator(1)
         salient(0)
+        logit(3, 2)
         ratio(1)
-        score(3, 3)
-        card_part(4, 2)
+        card_part(3, 0)
         logit(3, 1)
-        turn(0, 1)
-        coarse(2, 3)
+        turn(0, 0)
+        card_part(4, 0)
+        score(3, 3)
+        coarse(2, 1)
+        by_entity(1)
+        score(4, 0)
         coarse(2, 0)
-        logit(3, 0)
-        card_part(1, 3)
+        coarse(3, 2)
+        turn(0, 1)
+        card_codes(3)
+        by_mention(0, 0, 2048, "G")
         score(4, 1)
         peak(2)
-        card_part(4, 1)
-        score(4, 0)
-        turn(0, 0)
-        by_mention(0, 0, 2048, "G")
-        salient(1)
-        logit(3, 3)
-        card_part(4, 0)
-        logit(3, 2)
-        by_mention(1, 0, 2048, "G")
-        expo(2)
-        score(4, 2)
-        by_entity(1)
-        turn(1, 0)
-        turn(1, 1)
-        turn_copy(0, 1)
-        coarse(3, 2)
-        denominator(2)
-        coarse(3, 3)
         coarse(3, 1)
-        card_codes(4)
-        ratio(2)
-        coarse(3, 0)
-        score(6, 3)
-        logit(4, 2)
-        logit(4, 0)
-        logit(4, 1)
-        coarse(4, 2)
-        score(6, 0)
-        salient(2)
-        peak(3)
-        card_part(5, 0)
-        score(4, 3)
-        coarse(4, 1)
-        logit(4, 3)
-        by_mention(2, 0, 2048, "G")
-        by_entity(2)
-        score(6, 1)
-        expo(3)
-        card_part(5, 1)
-        turn_copy(0, 0)
-        score(6, 2)
-        coarse(4, 0)
-        denominator(3)
-        nil_share(0)
-        score(5, 0)
-        card_codes(1)
-        ratio(3)
-        logit(6, 1)
-        coarse(4, 3)
-        logit(6, 3)
-        turn_copy(1, 0)
-        logit(6, 0)
-        salient(3)
-        peak(4)
-        coarse(6, 3)
-        logit(6, 2)
-        coarse(6, 1)
-        score(5, 2)
+        logit(3, 0)
+        turn(1, 1)
+        score(4, 2)
         score(5, 1)
-        entity_quant(0)
+        turn(1, 0)
+        card_part(2, 2)
+        turn_copy(0, 1)
+        card_part(4, 2)
+        turn_copy(0, 0)
+        expo(2)
+        logit(3, 3)
+        score(4, 3)
+        coarse(3, 0)
         score(5, 3)
-        linked(0)
-        expo(4)
-        score(7, 2)
-        by_mention(3, 0, 2048, "G")
-        gather(0, 3, "S")
+        card_codes(2)
+        card_part(4, 3)
+        score(5, 2)
+        coarse(3, 3)
+        nil_share(1)
+        entity_quant(0)
         turn_copy(1, 1)
-        by_entity(3)
+        denominator(2)
+        logit(4, 0)
+        score(5, 0)
+        ratio(2)
+        logit(4, 1)
+        logit(4, 2)
+        linked(0)
+        score(6, 2)
+        card_part(4, 1)
+        salient(1)
+        peak(3)
+        logit(4, 3)
+        coarse(4, 1)
+        by_entity(2)
+        expo(3)
+        card_part(5, 0)
         turn(2, 1)
-        turn(2, 0)
-        logit(5, 1)
-        card_codes(5)
-        gather(0, 2, "S")
-        gather(0, 1, "S")
-        gather(0, 0, "S")
-        denominator(4)
+        denominator(3)
         logit(5, 2)
-        ratio(4)
-        gather_quant(0, 2)
         logit(5, 3)
-        logit(5, 0)
-        gather_quant(0, 1)
+        score(6, 1)
+        turn_copy(1, 0)
+        entity_quant(1)
         coarse(5, 3)
+        logit(5, 1)
+        coarse(4, 0)
+        logit(5, 0)
+        card_part(5, 2)
+        coarse(5, 2)
+        by_mention(1, 0, 2048, "G")
+        ratio(3)
+        card_codes(4)
+        linked(1)
+        turn_copy(2, 1)
+        coarse(4, 3)
+        salient(2)
+        coarse(4, 2)
+        by_entity(3)
+        coarse(5, 0)
+        coarse(5, 1)
+        turn(2, 0)
+        turn_copy(2, 0)
+        card_part(5, 3)
+        peak(4)
+        logit(6, 2)
+        score(6, 3)
+        by_mention(2, 0, 2048, "G")
+        peak(5)
+        salient(3)
+        score(6, 0)
+        turn(3, 0)
+        expo(4)
+        expo(5)
+        by_mention(3, 0, 2048, "G")
+        gather(0, 1, "V")
+        gather(0, 3, "V")
+        gather_quant(0, 1)
+        nil_share(2)
+        denominator(4)
+        coarse(6, 2)
         score(7, 1)
+        gather(0, 2, "S")
+        logit(6, 3)
+        denominator(5)
+        gather_quant(0, 3)
+        linked_out(1)
+        turn(3, 1)
+        coarse(6, 3)
+        score(7, 2)
+        logit(6, 1)
+        ratio(5)
+        logit(6, 0)
+        by_entity(5)
+        score(7, 3)
+        coarse(6, 1)
+        coarse(6, 0)
+        gather(0, 0, "S")
+        turn_copy(3, 0)
+        ratio(4)
+        card_part(5, 1)
+        entity_quant(2)
+        peak(6)
+        turn_copy(3, 1)
+        expo(6)
+        nil_share(0)
         by_entity(4)
         salient(4)
-        score(7, 3)
-        coarse(5, 0)
-        coarse(5, 2)
-        coarse(5, 1)
-        peak(5)
-        nil_share(3)
-        coarse(6, 2)
-        coarse(6, 0)
-        turn(3, 0)
-        logit(7, 3)
-        by_mention(4, 0, 2048, "G")
-        turn_copy(2, 1)
-        expo(5)
-        peak(6)
+        card_codes(5)
         logit(7, 1)
-        denominator(5)
-        coarse(7, 3)
-        ratio(5)
-        entity_quant(1)
-        nil_share(4)
-        turn(3, 1)
+        logit(7, 2)
+        salient(5)
+        coarse(7, 1)
+        by_mention(4, 0, 2048, "G")
+        logit(7, 3)
         score(7, 0)
         turn(4, 0)
-        by_entity(5)
-        nil_share(1)
-        expo(6)
-        logit(7, 0)
-        turn_copy(3, 1)
-        coarse(7, 1)
-        logit(7, 2)
         denominator(6)
-        turn_copy(3, 0)
-        turn(4, 1)
-        ratio(6)
-        gather_quant(0, 3)
-        linked(1)
-        coarse(7, 0)
-        salient(5)
-        entity_quant(3)
+        turn(5, 1)
+        logit(7, 0)
         coarse(7, 2)
-        peak(7)
+        ratio(6)
+        coarse(7, 3)
+        gather_quant(0, 0)
+        nil_share(3)
+        turn(4, 1)
+        coarse(7, 0)
+        linked(2)
+        turn(5, 0)
+        salient(6)
         by_mention(5, 0, 2048, "G")
-        linked_out(1)
+        nil_share(5)
+        entity_quant(3)
+        peak(7)
+        turn_copy(5, 1)
         linked_out(0)
         turn_copy(4, 0)
-        turn(5, 1)
         turn_copy(4, 1)
-        turn(5, 0)
-        linked(3)
-        entity_quant(4)
-        turn_copy(2, 0)
         expo(7)
-        entity_quant(2)
-        salient(6)
-        denominator(7)
-        ratio(7)
-        turn_copy(5, 1)
-        turn_copy(5, 0)
-        by_mention(6, 0, 2048, "G")
         by_entity(6)
-        salient(7)
-        by_mention(7, 2, 512, "S")
-        by_mention(7, 3, 512, "G")
-        entity_quant(5)
-        nil_share(2)
-        gather(1, 3, "S")
-        gather_quant(1, 3)
-        nil_share(5)
-        linked(2)
-        by_mention(7, 1, 512, "G")
-        turn(6, 1)
-        linked_out(3)
-        gather(1, 1, "S")
-        gather_quant(1, 1)
+        by_mention(6, 0, 2048, "G")
+        denominator(7)
+        linked(3)
+        ratio(7)
         turn(6, 0)
-        profile(12, "sc")
-        gather(1, 2, "S")
+        entity_quant(4)
+        turn_copy(5, 0)
+        entity_quant(5)
+        salient(7)
+        nil_share(7)
+        by_mention(7, 3, 512, "S")
+        linked(5)
+        by_mention(7, 0, 512, "G")
+        turn_copy(6, 0)
+        gather(1, 0, "S")
+        by_mention(7, 2, 512, "G")
+        turn(6, 1)
         linked_out(2)
-        gather_quant(1, 2)
-        profile(15, "sc")
-        profile(13, "acc")
-        gather_quant(0, 0)
-        profile_out(15, "S")
-        profile(4, "sc")
+        nil_share(6)
+        linked_out(3)
+        linked(4)
         by_entity(7)
-        profile(7, "sc")
-        profile_out(13, "S")
+        gather(1, 2, "S")
+        gather_quant(1, 0)
+        profile(2, "sc")
+        nil_share(4)
+        linked_out(4)
+        linked_out(5)
+        gather(1, 3, "V")
+        profile_out(2, "S")
+        profile(0, "sc")
+        profile(3, "acc")
+        gather_quant(1, 3)
         turn_copy(6, 1)
+        gather_quant(0, 2)
+        profile_out(0, "S")
+        profile_out(3, "S")
+        profile(1, "acc")
+        gather_quant(1, 2)
+        turn(7, 1)
+        turn(7, 0)
+        entity_quant(6)
+        profile(15, "sc")
+        profile(12, "sc")
+        profile(14, "sc")
+        profile_out(1, "S")
+        by_mention(7, 1, 512, "S")
+        profile(9, "sc")
+        profile_out(15, "S")
+        linked(6)
+        profile_out(12, "S")
+        profile(10, "sc")
+        gather(1, 1, "V")
+        profile_out(14, "S")
+        gather_quant(1, 1)
+        profile_out(9, "S")
+        linked_out(6)
+        turn_copy(7, 1)
+        profile(6, "acc")
+        turn_copy(7, 0)
+        profile(4, "sc")
+        entity_quant(7)
+        profile(11, "acc")
+        linked(7)
+        profile_out(6, "S")
+        profile(7, "sc")
+        profile(13, "acc")
+        profile(5, "sc")
+        profile_out(10, "S")
+        profile_out(11, "S")
         profile_out(4, "S")
         profile_out(7, "S")
-        profile(11, "acc")
-        linked(4)
-        profile_out(12, "S")
-        profile(14, "sc")
-        nil_share(6)
-        by_mention(7, 0, 512, "V")
-        linked_out(4)
-        profile(5, "sc")
-        turn_copy(6, 0)
-        profile_out(14, "S")
-        turn(7, 0)
-        profile_out(11, "S")
-        gather(1, 0, "S")
-        turn(7, 1)
-        gather_quant(1, 0)
+        profile_out(13, "S")
         profile(8, "acc")
-        profile_out(8, "S")
-        profile(10, "sc")
-        turn_copy(7, 0)
-        linked(5)
-        profile(1, "acc")
-        linked_out(5)
-        nil_share(7)
-        profile_out(10, "S")
-        turn_copy(7, 1)
-        profile(9, "sc")
-        entity_quant(7)
-        profile(3, "acc")
-        profile_out(1, "S")
-        entity_quant(6)
-        profile(0, "sc")
-        profile_out(5, "S")
-        profile_out(3, "S")
-        profile_out(0, "S")
-        linked(7)
         linked_out(7)
-        linked(6)
-        profile_out(9, "S")
-        profile(2, "sc")
-        profile_out(2, "S")
-        profile(6, "acc")
-        profile_out(6, "S")
-        linked_out(6)
+        profile_out(5, "S")
+        profile_out(8, "S")

from contextlib import ExitStack

import concourse.mybir as mybir
from concourse.masks import make_identity

M, E, K, D = 1024, 2048, 1024, 512
FLOPS = 2 * M * E * (K + D + D)

F32 = mybir.dt.float32
BF16 = mybir.dt.bfloat16
U32 = mybir.dt.uint32
U8 = mybir.dt.uint8
FP8 = mybir.dt.float8_e4m3fn
FP8X4 = mybir.dt.float8_e4m3fn_x4
ALU = mybir.AluOpType
ACT = mybir.ActivationFunctionType
ENG = mybir.EngineType

P = 128
G_M = M // 512
G_E = E // 512
KP = K // 512


def quantize(nc, codes, scales, grouped):
    nc.vector.quantize_mx(out=codes.bitcast(FP8X4), scales=scales, in_=grouped)


def tile_entity_linking_lift_f6_kernel(
    tc, mentions, entities_bytes, entities_scale, sharpness, prior, nil, rarity, salience,
    cards, contexts, nil_card, out_0, out_1,
):
    nc = tc.nc
    with ExitStack() as ctx:
        const = ctx.enter_context(tc.tile_pool(name="const", bufs=1))
        keep = ctx.enter_context(tc.tile_pool(name="keep", bufs=1))
        work = ctx.enter_context(tc.tile_pool(name="work", bufs=2))
        small = ctx.enter_context(tc.tile_pool(name="small", bufs=4))
        psum = ctx.enter_context(tc.psum_pool(name="psum", bufs=3))
        ctx.enter_context(tc.manual_schedule(engines={ENG.PE, ENG.Activation, ENG.DVE, ENG.Pool}))

        scale_b = const.tile([P, K], F32)
        sharp_h = const.tile([P, G_M, 4], BF16)
        nil_h = const.tile([P, G_M, 4], BF16)
        sal_h = const.tile([P, G_M, 4], BF16)
        nc.sync.dma_start(out=scale_b[:], in_=entities_scale.rearrange("o k -> (o k)").partition_broadcast(P))
        warm = const.tile([P, 1], F32)
        nc.vector.memset(warm[:], 0.0)
        nc.scalar.activation(out=warm[:], in_=warm[:], func=ACT.Exp)
        ident = const.tile([P, P], F32)
        make_identity(nc, ident[:])
        ebytes = []
        for c in range(G_E):
            eb = keep.tile([P, 4, K], U8, tag="eb", bufs=4)
            ebytes.append(eb)
        mraws = []
        for g in range(G_M):
            mraw = work.tile([P, 4, K], BF16, tag="big", bufs=4, align_bytes=64)
            mraws.append(mraw)

        def load_entities(c, j0, j1):
            rows = entities_bytes.rearrange("(r p) k -> p r k", p=P)
            nc.sync.dma_start(out=ebytes[c][:, j0:j1, :], in_=rows[:, 4 * c + j0 : 4 * c + j1, :])

        def load_mentions(g):
            nc.sync.dma_start(out=mraws[g][:], in_=mentions.rearrange("(g p t) k -> g p t k", p=P, t=4)[g])

        load_entities(0, 0, 1)
        load_entities(0, 1, 4)
        load_mentions(0)
        load_entities(1, 0, 4)
        prior_b = const.tile([P, E], BF16)
        rarity_b = const.tile([P, E], BF16)
        nilc_b = const.tile([P, D], BF16)
        nc.gpsimd.dma_start(out=sharp_h[:], in_=sharpness.rearrange("(g p t) -> p g t", p=P, t=4))
        nc.gpsimd.dma_start(out=nil_h[:], in_=nil.rearrange("(g p t) -> p g t", p=P, t=4))
        nc.gpsimd.dma_start(out=sal_h[:], in_=salience.rearrange("(g p t) -> p g t", p=P, t=4))
        load_entities(2, 0, 4)
        load_entities(3, 0, 4)
        nc.sync.dma_start(out=prior_b[:], in_=prior.partition_broadcast(P))

        sharp = const.tile([P, G_M * 4], F32)
        nilv = const.tile([P, G_M * 4], F32)
        nneg = const.tile([P, G_M * 4], F32)
        sal = const.tile([P, G_M * 4], F32)
        nc.gpsimd.tensor_copy(out=sharp[:], in_=sharp_h[:].rearrange("p g t -> p (g t)"))
        nc.gpsimd.tensor_copy(out=nilv[:], in_=nil_h[:].rearrange("p g t -> p (g t)"))
        nc.gpsimd.tensor_scalar(out=nneg[:], in0=nilv[:], scalar1=-1.0, scalar2=0.0, op0=ALU.mult, op1=ALU.add)
        nc.gpsimd.tensor_copy(out=sal[:], in_=sal_h[:].rearrange("p g t -> p (g t)"))

        craws = []
        for g in range(G_E + G_M):
            craw = work.tile([P, 4, D], BF16, tag="craw", bufs=3)
            source = cards if g < G_E else contexts
            nc.sync.dma_start(out=craw[:], in_=source.rearrange("(g p t) d -> g p t d", p=P, t=4)[g % G_E])
            craws.append(craw)
        nc.sync.dma_start(out=rarity_b[:], in_=rarity.partition_broadcast(P))
        load_mentions(1)
        nc.sync.dma_start(out=nilc_b[:], in_=nil_card.partition_broadcast(P))

        S = {}

        def transpose_rows(rows):
            words = rows.bitcast(F32)
            xt = psum.tile([P, KP, 2, P], F32, tag="tr", bufs=3)
            for c in range(KP):
                for u in range(2):
                    nc.tensor.transpose(xt[:, c, u, :], words[:, 256 * c + u : 256 * (c + 1) : 2], ident[:])
            return xt

        def copy_rows(xt, grouped):
            nc.scalar.copy(out=grouped, in_=xt[:].rearrange("p c u r -> p c r u"))

        mgs, mq, mqs = {}, {}, {}

        def mention_rows(g, t):
            if g not in mgs:
                mg = work.tile([P, 4, KP, P, 4], BF16, tag="big", bufs=4, align_bytes=64)
                mgs[g] = mg
            grouped = mgs[g][:, t].rearrange("p c r j -> p (c r j)").bitcast(F32).rearrange("p (c r u) -> p c r u", c=KP, u=2)
            S["mt", g, t] = transpose_rows(mraws[g][:, t, :]), grouped

        def mention_copy(g, t):
            copy_rows(*S["mt", g, t])

        def mention_codes(g):
            codes = keep.tile([P, 4 * KP * P], U32, tag="mq", bufs=2, align_bytes=64)
            scales = keep.tile([P, 4 * KP * P], U8, tag="mqs", bufs=2, align_bytes=64)
            quantize(nc, codes[:], scales[:], mgs[g][:].rearrange("p t c r j -> p (t c r j)"))
            mq[g], mqs[g] = codes, scales

        egs, xbs, eq, eqs = {}, {}, {}, {}

        def entity_scale(c, q):
            if c not in egs:
                eg = work.tile([P, KP, 4, P, 4], BF16, tag="big", bufs=4, align_bytes=64)
                egs[c] = eg
            xb = work.tile([P, K], BF16, tag="xb", bufs=3)
            nc.vector.tensor_tensor(out=xb[:], in0=ebytes[c][:, q, :].bitcast(FP8), in1=scale_b[:], op=ALU.mult)
            xbs[c, q] = xb

        def entity_rows(c, q):
            egw = egs[c][:].rearrange("p c q r j -> p (c q r j)").bitcast(F32).rearrange("p (c q r u) -> p c q r u", c=KP, q=4, u=2)
            S["et", c, q] = transpose_rows(xbs[c, q][:]), egw[:, :, q]

        def entity_copy(c, q):
            copy_rows(*S["et", c, q])

        def entity_codes(c):
            codes = keep.tile([P, KP * 512], U32, tag="eq", bufs=4, align_bytes=64)
            scales = keep.tile([P, KP * 512], U8, tag="eqs", bufs=4, align_bytes=64)
            quantize(nc, codes[:], scales[:], egs[c][:].rearrange("p c q r j -> p (c q r j)"))
            eq[c], eqs[c] = codes, scales

        cgs, cq, cqs = {}, {}, {}

        def card_part(g, part):
            if g not in cgs:
                cg = work.tile([P, D, 4], BF16, tag="grp", bufs=4, align_bytes=64)
                cgs[g] = cg
            cols = slice(part * 128, (part + 1) * 128)
            nc.scalar.copy(
                out=cgs[g][:, cols, :].rearrange("p (c i) t -> p c t i", i=4),
                in_=craws[g][:, :, cols].rearrange("p t (c i) -> p c t i", i=4),
            )

        def card_codes(g):
            codes = keep.tile([P, D], U32, tag="cq", bufs=6, align_bytes=64)
            scales = keep.tile([P, D], U8, tag="cqs", bufs=6, align_bytes=64)
            quantize(nc, codes[:], scales[:], cgs[g][:].rearrange("p d j -> p (d j)"))
            cq[g], cqs[g] = codes, scales

        bmq, bmqs, bmp = [], [], []
        for g in range(G_M):
            codes = keep.tile([P, E], U32, tag="bmq", bufs=2, align_bytes=64)
            scales = keep.tile([P, E], U8, tag="bmqs", bufs=2, align_bytes=64)
            bmq.append(codes)
            bmqs.append(scales)
            planes = work.tile([P, 4, E], BF16, tag="bmp", bufs=1)
            bmp.append(planes)

        def score(i, c):
            g, t = divmod(i, 4)
            sc = psum.tile([P, 512], F32, tag="sc", bufs=3)
            for k in range(KP):
                lo = (t * KP + k) * P
                nc.tensor.matmul_mx(
                    out=sc[:],
                    lhsT=mq[g][:, lo : lo + P].bitcast(FP8X4), lhsT_scale=mqs[g][:, lo : lo + P],
                    rhs=eq[c][:, k * 512 : (k + 1) * 512].bitcast(FP8X4), rhs_scale=eqs[c][:, k * 512 : (k + 1) * 512],
                    start=(k == 0), stop=(k == KP - 1),
                )
            S["sc", i, c] = sc

        def logit(i, c):
            if ("z", i) not in S:
                z = work.tile([P, E], F32, tag="z", bufs=3)
                zb = work.tile([P, E], BF16, tag="zb", bufs=2)
                S["z", i], S["zb", i] = z, zb
            cols = slice(c * 512, (c + 1) * 512)
            nc.vector.scalar_tensor_tensor(
                out=S["z", i][:, cols], in0=S["sc", i, c][:], scalar=sharp[:, i : i + 1],
                in1=prior_b[:, cols], op0=ALU.mult, op1=ALU.add,
            )

        def coarse(i, c):
            cols = slice(c * 512, (c + 1) * 512)
            nc.scalar.activation(out=S["zb", i][:, cols], in_=S["z", i][:, cols], func=ACT.Copy, scale=-1.0)

        def peak(i):
            zb = S["zb", i]
            negc = small.tile([P, 1], F32)
            nc.vector.tensor_scalar(out=zb[:], in0=zb[:], scalar1=1.0, scalar2=nneg[:, i : i + 1], op0=ALU.mult, op1=ALU.min, accum_out=negc[:])
            S["negc", i] = negc

        def expo(i):
            z, negc = S["z", i], S["negc", i]
            total = small.tile([P, 1], F32)
            en = small.tile([P, 1], F32)
            nc.scalar.activation(out=en[:], in_=nilv[:, i : i + 1], func=ACT.Exp, bias=negc[:])
            nc.scalar.activation(out=z[:], in_=z[:], func=ACT.Exp, bias=negc[:], accum_out=total[:])
            S["total", i], S["en", i] = total, en

        def denominator(i):
            den = small.tile([P, 1], F32)
            nc.vector.scalar_tensor_tensor(out=den[:], in0=S["total", i][:], scalar=1.0 / E, in1=S["en", i][:], op0=ALU.mult, op1=ALU.add)
            S["den", i] = den

        def ratio(i):
            rden = small.tile([P, 1], F32)
            nc.vector.reciprocal(out=rden[:], in_=S["den", i][:])
            S["rden", i] = rden

        def salient(i):
            fsal = small.tile([P, 1], F32)
            nc.gpsimd.tensor_tensor(out=fsal[:], in0=sal[:, i : i + 1], in1=S["rden", i][:], op=ALU.mult)
            S["fsal", i] = fsal

        def by_mention(i, j, n, eng):
            g, t = divmod(i, 4)
            z, fsal = S["z", i], S["fsal", i]
            cols = slice(j * n, (j + 1) * n)
            dst = bmp[g][:, t, cols]
            if eng == "G":
                nc.gpsimd.tensor_scalar(out=dst, in0=z[:, cols], scalar1=fsal[:], scalar2=0.0, op0=ALU.mult, op1=ALU.add)
            elif eng == "S":
                nc.scalar.activation(out=dst, in_=z[:, cols], func=ACT.Copy, scale=fsal[:])
            else:
                nc.vector.tensor_scalar(out=dst, in0=z[:, cols], scalar1=fsal[:], scalar2=None, op0=ALU.mult)

        def nil_share(i):
            pnil = small.tile([P, 1], F32)
            nc.gpsimd.tensor_tensor(out=pnil[:], in0=S["en", i][:], in1=S["rden", i][:], op=ALU.mult)
            S["pnil", i] = pnil

        def by_entity(i):
            be = work.tile([P, E], BF16, tag="be", bufs=2)
            nc.vector.scalar_tensor_tensor(
                out=be[:], in0=S["z", i][:], scalar=S["rden", i][:], in1=rarity_b[:], op0=ALU.mult, op1=ALU.mult,
            )
            S["be", i] = be

        def turn(i, h):
            if ("bg", i) not in S:
                bg = work.tile([P, G_E, P, 4], BF16, tag="grp", bufs=4, align_bytes=64)
                S["bg", i] = bg
            words = S["be", i][:].bitcast(F32)
            bgw = S["bg", i][:].rearrange("p c r j -> p (c r j)").bitcast(F32).rearrange("p (c r u) -> p c r u", c=G_E, u=2)
            xt = psum.tile([P, 2, 2, P], F32, tag="tr", bufs=3)
            for c in range(2):
                for u in range(2):
                    lo = 256 * (2 * h + c)
                    nc.tensor.transpose(xt[:, c, u, :], words[:, lo + u : lo + 256 : 2], ident[:])
            S["xt", i, h] = xt, bgw

        def turn_copy(i, h):
            xt, bgw = S["xt", i, h]
            nc.scalar.copy(out=bgw[:, 2 * h : 2 * h + 2], in_=xt[:].rearrange("p c u r -> p c r u"))

        def entity_quant(i):
            codes = work.tile([P, G_E * P], U32, tag="beq", bufs=2, align_bytes=64)
            scales = work.tile([P, G_E * P], U8, tag="beqs", bufs=2, align_bytes=64)
            quantize(nc, codes[:], scales[:], S["bg", i][:].rearrange("p c r j -> p (c r j)"))
            S["beq", i] = codes, scales

        def linked(i):
            codes, scales = S["beq", i]
            acc = psum.tile([P, D], F32, tag="acc", bufs=2)
            for c in range(G_E):
                nc.tensor.matmul_mx(
                    out=acc[:],
                    lhsT=codes[:, c * P : (c + 1) * P].bitcast(FP8X4), lhsT_scale=scales[:, c * P : (c + 1) * P],
                    rhs=cq[c][:].bitcast(FP8X4), rhs_scale=cqs[c][:],
                    start=(c == 0), stop=(c == G_E - 1),
                )
            S["acc", i] = acc

        def linked_out(i):
            g, t = divmod(i, 4)
            res = work.tile([P, D], F32, tag="res", bufs=4)
            nc.vector.scalar_tensor_tensor(out=res[:], in0=nilc_b[:], scalar=S["pnil", i][:], in1=S["acc", i][:], op0=ALU.mult, op1=ALU.add)
            nc.sync.dma_start(out=out_0.rearrange("(g p t) d -> g t p d", p=P, t=4)[g, t], in_=res[:])

        def gather(g, c, eng):
            bmi = work.tile([P, 512, 4], BF16, tag="grp", bufs=4, align_bytes=64)
            src = bmp[g][:, :, c * 512 : (c + 1) * 512].rearrange("p t (q i) -> p q t i", i=4)
            dst = bmi[:].rearrange("p (q i) t -> p q t i", i=4)
            if eng == "V":
                nc.vector.tensor_copy(out=dst, in_=src)
            else:
                nc.scalar.copy(out=dst, in_=src)
            S["bmi", g, c] = bmi

        def gather_quant(g, c):
            cols = slice(c * 512, (c + 1) * 512)
            quantize(nc, bmq[g][:, cols], bmqs[g][:, cols], S["bmi", g, c][:].rearrange("p e j -> p (e j)"))

        def profile(r, tag):
            acc = psum.tile([P, D], F32, tag=tag, bufs={"acc": 2, "sc": 3, "tr": 3}[tag])
            cols = slice(r * P, (r + 1) * P)
            for g in range(G_M):
                nc.tensor.matmul_mx(
                    out=acc[:],
                    lhsT=bmq[g][:, cols].bitcast(FP8X4), lhsT_scale=bmqs[g][:, cols],
                    rhs=cq[G_E + g][:].bitcast(FP8X4), rhs_scale=cqs[G_E + g][:],
                    start=(g == 0), stop=(g == G_M - 1),
                )
            S["prof", r] = acc

        def profile_out(r, eng):
            if ("wide", r // 4) not in S:
                wide = work.tile([P, 4, D], F32, tag="z", bufs=3)
                S["wide", r // 4] = wide
            res = S["wide", r // 4][:, r % 4, :]
            if eng == "S":
                nc.scalar.copy(out=res, in_=S["prof", r][:])
            else:
                nc.vector.tensor_copy(out=res, in_=S["prof", r][:])
            nc.sync.dma_start(out=out_1[r * P : (r + 1) * P, :], in_=res)

        entity_scale(0, 0)
        entity_scale(0, 1)
        entity_rows(0, 0)
        entity_scale(0, 2)
        entity_rows(0, 1)
        mention_rows(0, 0)
        entity_scale(0, 3)
        entity_copy(0, 0)
        entity_rows(0, 2)
        mention_copy(0, 0)
        mention_rows(0, 1)
        entity_rows(0, 3)
        entity_scale(1, 0)
        mention_rows(0, 3)
        entity_copy(0, 2)
        mention_rows(0, 2)
        entity_copy(0, 1)
        entity_scale(1, 2)
        entity_scale(1, 3)
        entity_rows(1, 0)
        mention_copy(0, 1)
        entity_rows(1, 3)
        entity_scale(1, 1)
        entity_rows(1, 2)
        entity_scale(2, 2)
        mention_copy(0, 3)
        entity_copy(1, 0)
        entity_scale(3, 3)
        entity_scale(2, 1)
        entity_copy(0, 3)
        entity_codes(0)
        mention_copy(0, 2)
        entity_copy(1, 2)
        entity_scale(3, 2)
        mention_codes(0)
        entity_rows(1, 1)
        entity_scale(2, 0)
        entity_rows(2, 2)
        card_part(0, 3)
        card_part(0, 0)
        entity_copy(1, 3)
        card_part(1, 0)
        entity_rows(3, 3)
        card_part(1, 3)
        entity_copy(1, 1)
        entity_scale(2, 3)
        card_part(0, 1)
        entity_rows(2, 1)
        card_part(2, 3)
        entity_rows(3, 2)
        entity_copy(2, 1)
        entity_scale(3, 0)
        score(0, 0)
        card_part(2, 1)
        entity_scale(3, 1)
        entity_rows(2, 0)
        entity_rows(2, 3)
        score(1, 0)
        logit(0, 0)
        entity_copy(3, 3)
        entity_copy(3, 2)
        entity_rows(3, 0)
        mention_rows(1, 1)
        entity_codes(1)
        card_part(0, 2)
        entity_rows(3, 1)
        score(0, 1)
        mention_rows(1, 3)
        entity_copy(2, 2)
        entity_copy(2, 3)
        card_part(1, 1)
        entity_copy(2, 0)
        entity_copy(3, 0)
        entity_codes(2)
        score(1, 1)
        logit(0, 1)
        card_part(2, 0)
        logit(1, 0)
        score(0, 2)
        entity_copy(3, 1)
        entity_codes(3)
        card_part(3, 1)
        mention_copy(1, 1)
        logit(0, 2)
        mention_rows(1, 2)
        card_codes(0)
        mention_rows(1, 0)
        coarse(0, 0)
        score(0, 3)
        score(1, 3)
        score(1, 2)
        logit(0, 3)
        logit(1, 1)
        logit(1, 3)
        score(2, 2)
        coarse(0, 1)
        mention_copy(1, 3)
        score(2, 3)
        coarse(1, 0)
        card_part(1, 2)
        logit(1, 2)
        mention_copy(1, 2)
        logit(2, 2)
        card_part(3, 3)
        score(2, 0)
        score(2, 1)
        coarse(0, 3)
        mention_copy(1, 0)
        coarse(0, 2)
        score(3, 1)
        coarse(1, 2)
        peak(0)
        coarse(1, 3)
        score(3, 0)
        logit(2, 0)
        logit(2, 3)
        coarse(1, 1)
        expo(0)
        card_codes(1)
        card_part(3, 2)
        peak(1)
        denominator(0)
        coarse(2, 2)
        score(3, 2)
        logit(2, 1)
        expo(1)
        coarse(2, 3)
        ratio(0)
        mention_codes(1)
        by_entity(0)
        denominator(1)
        salient(0)
        logit(3, 2)
        ratio(1)
        card_part(3, 0)
        logit(3, 1)
        turn(0, 0)
        card_part(4, 0)
        score(3, 3)
        coarse(2, 1)
        by_entity(1)
        score(4, 0)
        coarse(2, 0)
        coarse(3, 2)
        turn(0, 1)
        card_codes(3)
        by_mention(0, 0, 2048, "G")
        score(4, 1)
        peak(2)
        coarse(3, 1)
        logit(3, 0)
        turn(1, 1)
        score(4, 2)
        score(5, 1)
        turn(1, 0)
        card_part(2, 2)
        turn_copy(0, 1)
        card_part(4, 2)
        turn_copy(0, 0)
        expo(2)
        logit(3, 3)
        score(4, 3)
        coarse(3, 0)
        score(5, 3)
        card_codes(2)
        card_part(4, 3)
        score(5, 2)
        coarse(3, 3)
        nil_share(1)
        entity_quant(0)
        turn_copy(1, 1)
        denominator(2)
        logit(4, 0)
        score(5, 0)
        ratio(2)
        logit(4, 1)
        logit(4, 2)
        linked(0)
        score(6, 2)
        card_part(4, 1)
        salient(1)
        peak(3)
        logit(4, 3)
        coarse(4, 1)
        by_entity(2)
        expo(3)
        card_part(5, 0)
        turn(2, 1)
        denominator(3)
        logit(5, 2)
        logit(5, 3)
        score(6, 1)
        turn_copy(1, 0)
        entity_quant(1)
        coarse(5, 3)
        logit(5, 1)
        coarse(4, 0)
        logit(5, 0)
        card_part(5, 2)
        coarse(5, 2)
        by_mention(1, 0, 2048, "G")
        ratio(3)
        card_codes(4)
        linked(1)
        turn_copy(2, 1)
        coarse(4, 3)
        salient(2)
        coarse(4, 2)
        by_entity(3)
        coarse(5, 0)
        coarse(5, 1)
        turn(2, 0)
        turn_copy(2, 0)
        card_part(5, 3)
        peak(4)
        logit(6, 2)
        score(6, 3)
        by_mention(2, 0, 2048, "G")
        peak(5)
        salient(3)
        score(6, 0)
        turn(3, 0)
        expo(4)
        expo(5)
        by_mention(3, 0, 2048, "G")
        gather(0, 1, "V")
        gather(0, 3, "V")
        gather_quant(0, 1)
        nil_share(2)
        denominator(4)
        coarse(6, 2)
        score(7, 1)
        gather(0, 2, "S")
        logit(6, 3)
        denominator(5)
        gather_quant(0, 3)
        linked_out(1)
        turn(3, 1)
        coarse(6, 3)
        score(7, 2)
        logit(6, 1)
        ratio(5)
        logit(6, 0)
        by_entity(5)
        score(7, 3)
        coarse(6, 1)
        coarse(6, 0)
        gather(0, 0, "S")
        turn_copy(3, 0)
        ratio(4)
        card_part(5, 1)
        entity_quant(2)
        peak(6)
        turn_copy(3, 1)
        expo(6)
        nil_share(0)
        by_entity(4)
        salient(4)
        card_codes(5)
        logit(7, 1)
        logit(7, 2)
        salient(5)
        coarse(7, 1)
        by_mention(4, 0, 2048, "G")
        logit(7, 3)
        score(7, 0)
        turn(4, 0)
        denominator(6)
        turn(5, 1)
        logit(7, 0)
        coarse(7, 2)
        ratio(6)
        coarse(7, 3)
        gather_quant(0, 0)
        nil_share(3)
        turn(4, 1)
        coarse(7, 0)
        linked(2)
        turn(5, 0)
        salient(6)
        by_mention(5, 0, 2048, "G")
        nil_share(5)
        entity_quant(3)
        peak(7)
        turn_copy(5, 1)
        linked_out(0)
        turn_copy(4, 0)
        turn_copy(4, 1)
        expo(7)
        by_entity(6)
        by_mention(6, 0, 2048, "G")
        denominator(7)
        linked(3)
        ratio(7)
        turn(6, 0)
        entity_quant(4)
        turn_copy(5, 0)
        entity_quant(5)
        salient(7)
        nil_share(7)
        by_mention(7, 3, 512, "S")
        linked(5)
        by_mention(7, 0, 512, "G")
        turn_copy(6, 0)
        gather(1, 0, "S")
        by_mention(7, 2, 512, "G")
        turn(6, 1)
        linked_out(2)
        nil_share(6)
        linked_out(3)
        linked(4)
        by_entity(7)
        gather(1, 2, "S")
        gather_quant(1, 0)
        profile(2, "sc")
        nil_share(4)
        linked_out(4)
        linked_out(5)
        gather(1, 3, "V")
        profile_out(2, "S")
        profile(0, "sc")
        profile(3, "acc")
        gather_quant(1, 3)
        turn_copy(6, 1)
        gather_quant(0, 2)
        profile_out(0, "S")
        profile_out(3, "S")
        profile(1, "acc")
        gather_quant(1, 2)
        turn(7, 1)
        turn(7, 0)
        entity_quant(6)
        profile(15, "sc")
        profile(12, "sc")
        profile(14, "sc")
        profile_out(1, "S")
        by_mention(7, 1, 512, "S")
        profile(9, "sc")
        profile_out(15, "S")
        linked(6)
        profile_out(12, "S")
        profile(10, "sc")
        gather(1, 1, "V")
        profile_out(14, "S")
        gather_quant(1, 1)
        profile_out(9, "S")
        linked_out(6)
        turn_copy(7, 1)
        profile(6, "acc")
        turn_copy(7, 0)
        profile(4, "sc")
        entity_quant(7)
        profile(11, "acc")
        linked(7)
        profile_out(6, "S")
        profile(7, "sc")
        profile(13, "acc")
        profile(5, "sc")
        profile_out(10, "S")
        profile_out(11, "S")
        profile_out(4, "S")
        profile_out(7, "S")
        profile_out(13, "S")
        profile(8, "acc")
        linked_out(7)
        profile_out(5, "S")
        profile_out(8, "S")
